import numpy as np, ml_dtypes
CORES = [24,25,26,27,28,29,30,31]
N = 8
import mx_ref
BF = ml_dtypes.bfloat16
def cols(t, e):
    v = np.concatenate([t.reshape(128, -1, 4), np.zeros((128, 1, 4), BF)], axis=1)
    return np.ascontiguousarray(v[:, e]).reshape(128, -1)
def cut(t, i, w=512):
    return t[:, w * i:w * i + w]
def tile(rs):
    return np.stack(rs, axis=2).reshape(128, -1).astype(BF)
def pick(q, e):
    c = np.concatenate([q[0].reshape(128, -1, 4), np.zeros((128, 1, 4), np.uint8)], axis=1); s = np.concatenate([q[1], np.ones((16, 1), np.uint8)], axis=1)
    return (np.ascontiguousarray(c[:, e].reshape(128, -1)), np.ascontiguousarray(s[:, e]))
def join(*qs):
    return (np.concatenate([q[0] for q in qs], axis=1), np.concatenate([q[1] for q in qs], axis=1))
def put(q, e, v):
    c, s = q[0].reshape(128, -1, 4).copy(), q[1].copy(); c[:, e] = v[0].reshape(128, -1, 4); s[:, e] = v[1]
    return (c.reshape(128, -1), s)
def pk(c, s):
    return (np.ascontiguousarray(c), mx_ref.live(s))
def emit(q):
    return q[0], q[1]
def decode(q):
    o = []
    for b in range(4):
        e = np.zeros((128, 128, 4), np.float32); e[np.arange(128), np.arange(128), b] = 1
        o.append(mx_ref.matmul(mx_ref.quantize(e.reshape(128, 512).astype(BF)), q))
    return np.stack(o, axis=2).reshape(128, -1)
def f(rng, *shape):
    return mx_ref.flush((rng.standard_normal(shape, dtype=np.float32) * np.exp2(rng.integers(-2, 3, shape[:-1] + (1,)))).astype(BF))
def wide(rng, *shape, cols=0):
    v = rng.standard_normal(shape, dtype=np.float32) * np.exp2(rng.integers(-12, 13, shape)).astype(np.float32)
    if cols: v *= np.repeat(np.exp2(rng.integers(-cols, cols + 1, shape[:-2] + (1, shape[-1] // 4))) * (rng.random(shape[:-2] + (1, shape[-1] // 4)) > 0.0625), 4, axis=-1).astype(np.float32)
    return mx_ref.flush(v.astype(BF))
T, CAPP, CAPR = 128, 48, 16
def big(v, k):
    v = v.astype(np.float32) * np.float32(k)
    v[np.abs(v) < np.float32(2.0 ** -6)] = 0
    return v.astype(BF)
def same(t):
    return np.repeat(t[None], N, axis=0)
def only(t, k):
    t = np.array(t)
    t[:, 4 * k:] = 0
    return t
def plain(rng):
    return {"x": f(rng, N, 128, 4 * T), "gr": big(f(rng, N, 128, 4 * T), 8), "rt": same(only(f(rng, 128, 512), N)), "w": f(rng, N, 128, 2048), "ub": big(f(rng, N, 128, 2048), 4), "pr": same(only(f(rng, 128, 512), 1)), "v": f(rng, N, 128, 512)}
def deal(rng, n, among):
    m, j, p = len(among), np.arange(n), rng.permutation(among)
    return np.stack([p[j % m], p[(j + 1 + j // m % (m - 1)) % m]], axis=1)
def routed(rng, to, far=False):
    g = np.arange(128) // (128 // N)
    rt = np.zeros((128, 128, 4), np.float32)
    rt[np.arange(128), g, 0] = 1 + rng.random(128)
    x = rng.standard_normal((N, 128, T, 4)) * (2 if far else 8)
    low = 0.125 * rng.choice([-1.0, 1.0], (N, 128, T))
    first, second = to[:, None, :, 0] == g[None, :, None], to[:, None, :, 1] == g[None, :, None]
    size = np.where(first, low, np.where(second, -4.0, -16.0)) if far else np.where(first, 16.0, np.where(second, 2.0, low))
    x[..., 0] = size * (1 + rng.random((N, 128, T)))
    if far: x, rt = x * 2.0 ** 25, rt * np.float32(2.0 ** 29)
    return {"x": mx_ref.flush(x.reshape(N, 128, 4 * T).astype(np.float32).astype(BF)), "rt": same(rt.reshape(128, 512).astype(BF))}
def setup_inputs(rng):
    return plain(rng)
def setup_inputs_crowd(rng):
    h = int(rng.integers(0, N))
    rest, n, to = np.delete(np.arange(N), h), [CAPP, T, CAPP + 1, CAPR, 0, CAPR + 1, CAPR - 1, 1], np.zeros((N, T, 2), int)
    for i in range(N):
        t = deal(rng, T, rest)
        t[np.arange(n[i]), rng.integers(0, 2, n[i])] = h
        to[(h + 1 + i) % N] = t[rng.permutation(T)]
    d = {**plain(rng), **routed(rng, to)}
    sign, pr = rng.choice([-1.0, 1.0], (128, 1, 4)), np.zeros((128, 128, 4), np.float32)
    pr[:, :1] = 2.0 ** 29 * sign * (1 + rng.random((128, 1, 4)))
    gr = 2.0 ** 28 * sign[None] * (1 + rng.random((N, 128, T, 4))) * rng.choice([-1.0, 1.0], (N, 1, T, 1))
    d["pr"] = same(pr.reshape(128, 512).astype(BF))
    d["gr"] = gr.reshape(N, 128, 4 * T).astype(np.float32).astype(BF)
    d["ub"] = (d["ub"].astype(np.float32) * np.float32(2.0 ** -22)).astype(BF)
    return d
def setup_inputs_dead(rng):
    rest = np.delete(np.arange(N), int(rng.integers(0, N)))
    to, dead = np.zeros((N, T, 2), int), np.zeros((N, T), bool)
    for q in range(N):
        s = rng.permutation(T)
        to[q] = deal(rng, T, rest)[s]
        dead[q] = s // (N - 1) % 4 != 0
    d = {**plain(rng), **routed(rng, to)}
    x = d["x"].astype(np.float32).reshape(N, 128, T, 4)
    x[..., 1:] = 16 * (1 + rng.random((N, 128, T, 3))) * np.where(dead, 1.0, -1.0)[:, None, :, None]
    d["x"] = x.reshape(N, 128, 4 * T).astype(BF)
    w = np.array(d["w"])
    w[rng.permutation(rest)[:N // 2]] = (-1 - rng.random((N // 2, 128, 2048))).astype(np.float32).astype(BF)
    d["w"] = w
    return d
def setup_inputs_one(rng):
    h = int(rng.integers(0, N))
    to = np.full((N, T, 2), h)
    for q in range(N): to[q, :, 1] = rng.permutation(deal(rng, T, np.delete(np.arange(N), h))[:, 0])
    return {**plain(rng), **routed(rng, to, far=True)}
def setup_inputs_spread(rng):
    d = plain(rng)
    x = (wide(rng, N, 128, 4 * T, cols=6).astype(np.float32) * np.float32(2.0 ** 8)).reshape(N, 128, T, 4)
    for q in range(N):
        i = rng.permutation(T)[:T // 8]
        x[q][:, i] = 2.0 ** -29 * (1 + rng.random((128, i.size, 4))) * rng.choice([-1.0, 1.0], (128, i.size, 4))
    d["x"] = x.reshape(N, 128, 4 * T).astype(BF)
    d["rt"] = (d["rt"].astype(np.float32) * np.float32(2.0 ** 20)).astype(BF)
    d["gr"] = big(wide(rng, N, 128, 4 * T, cols=3), 16)
    return d
def setup_inputs_ties(rng):
    u, o = sorted(rng.permutation(N)[:2].tolist())
    rest = np.delete(np.arange(N), [u, o])
    to, at = np.zeros((N, T, 2), int), []
    for q in range(N):
        t, s = deal(rng, T, rest), rng.permutation(T)
        t[:T // 2] = np.array([u, rest[0]])
        t[T // 2:T // 2 + 4, 1] = u
        to[q] = t[s]
        at.append(np.flatnonzero(s < T // 2))
    d = {**plain(rng), **routed(rng, to)}
    r = np.array(d["rt"]).reshape(N, 128, 128, 4)
    r[:, :, o] = r[:, :, u]
    x, g = d["x"].astype(np.float32).reshape(N, 128, T, 4), d["gr"].astype(np.float32).reshape(N, 128, T, 4)
    for q in range(N):
        i = at[q]
        x[q][:, i] = x[q][:, i[:1]].copy()
        g[q][:, i] = g[q][:, i[:1]].copy() * rng.choice([-1.0, 1.0], i.size)[None, :, None]
    return {**d, "x": x.reshape(N, 128, 4 * T).astype(BF), "gr": g.reshape(N, 128, 4 * T).astype(BF), "rt": r.reshape(N, 128, 512)}
def check_inputs(d):
    b = []
    for k in ("x", "gr", "rt", "w", "ub", "pr", "v"):
        a = np.abs(d[k].astype(np.float32))
        if not (np.isfinite(a).all() and ((a == 0) | (a >= 2.0 ** -30) & (a <= 2.0 ** 30)).all()): b.append("a value of " + k)
    for k, n in (("rt", N), ("pr", 1)):
        a = d[k].astype(np.float32)
        if (a != a[:1]).any(): b.append(k + " differs between ranks")
        if (a[:, :, 4 * n:] != 0).any(): b.append(k + " has numbers behind its first columns")
    return b
def reference(x, gr, rt, w, ub, pr, v):
    qz = lambda t: mx_ref.quantize(np.ascontiguousarray(t))
    to = []
    for q in range(N):
        s = mx_ref.matmul(qz(rt[q]), qz(x[q]))[:N] + np.float32(0)
        to.append(np.argsort(-s, axis=0, kind="stable")[:2])
    everyx, everyg = np.concatenate([x[q] for q in range(N)], axis=1), np.concatenate([gr[q] for q in range(N)], axis=1)
    came = np.zeros((N, 128, 2 * T, 4), np.float32)
    ct = np.zeros((N, 1, T), np.float32)
    for e in range(N):
        taken = [np.flatnonzero((to[q] == e).any(axis=0))[:CAPP] for q in range(N)]
        at = np.full((N, CAPP), -1)
        for q in range(N): at[q, :taken[q].size] = T * q + taken[q]
        at = at.reshape(-1)
        xs, gs = qz(cols(everyx, at)), qz(cols(everyg, at))
        forward = np.stack([mx_ref.matmul(qz(cut(w[e], i)), xs) for i in range(4)], axis=2).reshape(128, -1)
        m = qz(np.where(forward > 0, decode(gs), np.float32(0)).astype(BF))
        strength = np.abs(mx_ref.matmul(qz(pr[e]), m)[0])
        dx = decode(qz(tile([mx_ref.matmul(qz(cut(ub[e], i)), m) * np.float32(0.0625) for i in range(4)]))).reshape(128, -1, 4)
        for q in range(N):
            k = np.argsort(-strength[CAPP * q:CAPP * q + taken[q].size], kind="stable")[:CAPR]
            j = taken[q][k]
            second = (to[q][1, j] == e).astype(int)
            came[q][:, T * second + j] = dx[:, CAPP * q + k]
            ct[q, 0, j] += 1 + second
    oc, osc, y = np.zeros((N, 128, 4 * T), np.uint8), np.zeros((N, 16, T), np.uint8), np.zeros((N, 128, T), np.float32)
    for q in range(N):
        z = qz((came[q][:, :T] + came[q][:, T:]).reshape(128, 4 * T).astype(BF))
        oc[q], osc[q] = emit(z)
        y[q] = mx_ref.matmul(qz(v[q]), z)
    return {"oc": oc, "osc": osc, "ct": ct, "y": y}

@@ -1,0 +1,467 @@
+from concourse.bass import DstId, RemoteDMATransfer
+from concourse.mybir import dt, AluOpType, AxisListType, ActivationFunctionType
+
+A = AluOpType
+F = ActivationFunctionType
+BIG, TINY, MAGIC16, MAGIC1 = 1e29, 2.0 ** -100, 1.5 * 2.0 ** 27, 1.5 * 2.0 ** 23
+
+SCRATCH = {}
+ALIAS = {}
+
+
+def _sb(name, n, d="float32"):
+    SCRATCH[name] = ("sbuf", [128, n], d)
+
+
+def _mx(name, n):
+    _sb(name, n, "float8_e4m3fn_x4")
+    _sb(name + "_s", n, "uint8")
+
+
+for _n, _w in (("xq", 400), ("rlq", 264), ("tkq", 128), ("rq", 128), ("sl", 768), ("ld", 768), ("xe", 384), ("ge", 384), ("wq", 512),
+               ("uq", 512), ("vq", 128), ("prq", 128), ("ebq", 512), ("mq", 384), ("dxw", 516), ("blq", 136), ("ret", 256), ("rl", 288),
+               ("kq", 128), ("ahq", 256), ("ohq", 128), ("btq", 160), ("zc", 256), ("zq", 128)):
+    _mx(_n, _w)
+for _n, _w in (("xt", 544), ("gt", 544), ("rlt", 1056), ("tk", 512), ("bt", 512), ("rst", 512), ("wb", 2048), ("ubb", 2048), ("vb", 512),
+               ("pb", 4), ("prt", 512), ("ebt", 2048), ("mt", 1536), ("dxt", 1536), ("blt", 544), ("at", 528), ("kt", 512), ("aht", 1024),
+               ("oht", 512), ("bt2", 640), ("zt", 512), ("zer", 512), ("ones", 128), ("ti", 128), ("e128", 128), ("rp", 128), ("tmpc", 128),
+               ("wt", 128), ("oh", 384), ("mk", 1536), ("sg", 768), ("junk", 384), ("mka", 48), ("mkh", 48)):
+    _sb(_n, _w, "bfloat16")
+for _n, _w in (("sc", 16), ("cc", 288), ("pm", 16), ("pm2", 16), ("cm", 16), ("ab", 8), ("s2", 8), ("iab", 4),
+               ("acc", 4), ("n48", 48), ("ys", 96), ("t96", 96), ("dd", 288), ("cmp", 288), ("rk", 4), ("tok", 4), ("mm_", 4), ("rr_", 4),
+               ("wk", 4), ("cd", 4), ("rkh", 4), ("rth", 4), ("rrh", 4), ("ysb", 128), ("ctsb", 128)):
+    _sb(_n, _w)
+_at = 0
+for _n, _w in (("em16", 16), ("emv", 16), ("g48", 48), ("bi", 16), ("bib", 16), ("si8", 16), ("cp16", 16), ("s96", 96), ("h96", 96),
+               ("o96", 96), ("fx", 32), ("z8", 16)):
+    ALIAS[_n] = ("cs", _at)
+    _at += _w
+_sb("cs", _at)
+_sb("pi", 4, "int32")
+for _n, _w in (("off", 48), ("ofx", 24), ("ofg", 24), ("of2", 16), ("of3", 16)):
+    _sb(_n, _w, "uint16")
+for _k in range(8):
+    SCRATCH["ps%d" % _k] = ("psum", [128, 512], "float32")
+SEMAPHORES = ["sv", "ss", "st", "sg", "lx", "lrt", "lgr", "lpr", "lw", "lub", "lv", "arc", "arp", "owc", "owp", "rec", "rep", "orc", "orp",
+              "loc", "o_oc", "o_y", "o_ct", "o_s0", "o_s1", "o_s2", "o_s3"]
+
+
+def rank_program(g, core, T, topo):
+    q = T.rank_of(core)
+    if q is None:
+        return
+    N = len(T.cores)
+    eng = {"v": g.vector, "s": g.scalar, "t": g.tensor, "g": g, "y": g.sync}
+    own = {"v": "sv", "s": "ss", "t": "st", "g": "sg"}
+    total, snaps, log = {}, {}, {}
+    seen = {k: {} for k in eng}
+
+    def clash(a, b):
+        if a[2] <= b[1] or b[2] <= a[1]:
+            return False
+        return not (a[3] == b[3] > 1 and (a[1] - b[1]) % a[3])
+
+    def wait(qn, s, v):
+        if seen[qn].get(s, 0) >= v:
+            return
+        eng[qn].wait_ge(T.sem[s], v)
+        seen[qn][s] = v
+        for k, w in snaps.get((s, v), {}).items():
+            seen[qn][k] = max(seen[qn].get(k, 0), w)
+
+    def depend(qn, reads, writes, dma=False):
+        need = {}
+        for acc, w in [(r, False) for r in reads] + [(r, True) for r in writes]:
+            bank = acc[0][:2] == "ps" and len(acc[0]) == 3
+            for rec in log.get(acc[0], []):
+                if not bank and not clash(acc, rec[0]):
+                    continue
+                if not (w or rec[1] or (bank and rec[2] != qn)):
+                    continue
+                if rec[2] == qn and not dma and (not rec[1] or (qn == "t" and bank)):
+                    continue
+                need[rec[3]] = max(need.get(rec[3], 0), rec[4])
+        for s, v in need.items():
+            wait(qn, s, v)
+
+    def note(who, reads, writes, s, v):
+        for r in writes:
+            if r[3] == 1:
+                log[r[0]] = [k for k in log.get(r[0], []) if not (r[1] <= k[0][1] and k[0][2] <= r[2])]
+        for acc, w in [(r, False) for r in reads] + [(r, True) for r in writes]:
+            log.setdefault(acc[0], []).append((acc, w, who, s, v))
+
+    def op(qn, reads, writes, call):
+        depend(qn, reads, writes)
+        s = own[qn]
+        call().then_inc(T.sem[s], 1)
+        total[s] = total.get(s, 0) + 1
+        snaps[(s, total[s])] = dict(seen[qn])
+        note(qn, reads, writes, s, total[s])
+
+    def dma(qn, reads, writes, out, in_, s):
+        depend(qn, reads, writes, dma=True)
+        eng[qn].dma_start(out, in_).then_inc(T.sem[s], 16)
+        total[s] = total.get(s, 0) + 16
+        snaps[(s, total[s])] = dict(seen[qn])
+        note("dma", reads, writes, s, total[s])
+
+    def R(name, lo, hi, step=1):
+        b, o = ALIAS.get(name, (name, 0))
+        return (b, lo + o, hi + o, step)
+
+    def ap(r):
+        return T[r[0]][:, r[1]:r[2]] if r[3] == 1 else T[r[0]][:, r[1]:r[2]:r[3]]
+
+    def sc_(v):
+        return ap(v) if isinstance(v, tuple) else v
+
+    def rds(*vs):
+        return [v for v in vs if isinstance(v, tuple)]
+
+    def ts(out, in0, s1, s2, op0, op1=None):
+        if op1 is None:
+            op("v", rds(in0, s1), [out], lambda: g.vector.tensor_scalar(ap(out), ap(in0), sc_(s1), None, op0))
+        else:
+            op("v", rds(in0, s1, s2), [out], lambda: g.vector.tensor_scalar(ap(out), ap(in0), sc_(s1), sc_(s2), op0, op1))
+
+    def tt(out, a, b, o):
+        op("v", [a, b], [out], lambda: g.vector.tensor_tensor(ap(out), ap(a), ap(b), o))
+
+    def cp(out, a):
+        op("v", [a], [out], lambda: g.vector.tensor_copy(ap(out), ap(a)))
+
+    def ms(out, c):
+        op("v", [], [out], lambda: g.vector.memset(ap(out), c))
+
+    def red(out, a, o):
+        op("v", [a], [out], lambda: g.vector.tensor_reduce(ap(out), ap(a), AxisListType.X, o))
+
+    def scan(out, a, z):
+        op("v", [a, z], [out], lambda: g.vector.tensor_tensor_scan(ap(out), ap(a), ap(z), -9e29, A.max, A.add))
+
+    def qz(name, lo, n, tile, t0=0):
+        op("v", [R(tile, t0, t0 + 4 * n)], [R(name, lo, lo + n), R(name + "_s", lo, lo + n)],
+           lambda: g.vector.quantize_mx(T[name][:, lo:lo + n], T[name + "_s"][:, lo:lo + n], T[tile][:, t0:t0 + 4 * n]))
+
+    def act(out, a, f, scale=1.0, bias=0.0, acc=None):
+        if acc is None:
+            op("s", rds(a, scale, bias), [out], lambda: g.scalar.activation(ap(out), ap(a), f, bias=sc_(bias), scale=sc_(scale)))
+        else:
+            op("s", rds(a, scale, bias), [out, acc],
+               lambda: g.scalar.activation(ap(out), ap(a), f, bias=sc_(bias), scale=sc_(scale), accum_out=ap(acc)))
+
+    def mm(bank, lhs, l0, rhs, r0, n, start=True, stop=True):
+        op("t", [R(lhs, l0, l0 + 128), R(lhs + "_s", l0, l0 + 128), R(rhs, r0, r0 + n), R(rhs + "_s", r0, r0 + n)], [R(bank, 0, n)],
+           lambda: g.tensor.matmul_mx(T[bank][:, 0:n], T[lhs][:, l0:l0 + 128], T[lhs + "_s"][:, l0:l0 + 128],
+                                      T[rhs][:, r0:r0 + n], T[rhs + "_s"][:, r0:r0 + n], start, stop))
+
+    def pick(out, o0, n, win, w1, off, f0):
+        fr = R(off, f0, f0 + n // 16)
+        op("v", [R(win, 0, w1), fr], [R(out, o0, o0 + n)],
+           lambda: g.vector.tensor_copy(T[out][:, o0:o0 + n].bitcast(dt.uint32), T[win][:, 0:w1].bitcast(dt.uint32).indirect(ap(fr))))
+        op("s", [R(win + "_s", 0, w1), fr], [R(out + "_s", o0, o0 + n)],
+           lambda: g.scalar.activation(T[out + "_s"][:, o0:o0 + n], T[win + "_s"][:, 0:w1].indirect(ap(fr)), F.Copy))
+
+    def iota(name, n, pattern, cm=0):
+        r = R(name, 0, n)
+        op("g", [], [r], lambda: g.iota(ap(r), pattern, 0, cm, allow_small_or_imprecise_dtypes=True))
+
+    peers = [c for c in T.cores if c != core]
+    far = [c for c in peers if topo.die(c) != topo.die(core)]
+    near = [c for c in peers if c not in far]
+    masks = {}
+    for group, first in ((far, 0), (near, 1)):
+        for j, c in enumerate(group):
+            e = topo.engines(core, c)[first::2]
+            masks[c] = (1 << e[2 * j]) | (1 << e[2 * j + 1])
+
+    def send(src, sw, width, dst, dw, s, code):
+        depend("g", [R(src, 0, sw * N)], [])
+        ts_ = []
+        for c in peers:
+            e = T.rank_of(c)
+            rid, pid = topo.addr(c)[:2]
+            a, b = T[src][:, sw * e:sw * e + width], T[dst][:, dw * q:dw * q + width]
+            if code:
+                a, b = a.bitcast(dt.uint8), b.bitcast(dt.uint8)
+            ts_.append(RemoteDMATransfer(dst_ids=[DstId(rid=rid, pnc=pid)], dma_engine_mask=masks[c], remote_sem=T.sem[s], src=a, dst=b))
+        g.remote_dma_fused(ts_, local_sem=T.sem["loc"])
+        total["loc"] = total.get("loc", 0) + 2 * len(peers)
+        note("dma", [R(src, 0, sw * N)], [], "loc", total["loc"])
+
+    def arrives(dst, dw, s):
+        total[s] = 2 * len(peers)
+        for e in range(N):
+            if e != q:
+                note("dma", [], [R(dst, dw * e, dw * (e + 1))], s, total[s])
+
+    def localcopy(src, a, dst, b, width, s, code):
+        i, o = T[src][:, a:a + width], T[dst][:, b:b + width]
+        if code:
+            i, o = i.bitcast(dt.uint8), o.bitcast(dt.uint8)
+        dma("y", [R(src, a, a + width)], [R(dst, b, b + width)], o, i, s)
+
+    def load(qn, name, w, src, s, at=0):
+        dma(qn, [], [R(name, at, at + w)], T[name][:, at:at + w], src, s)
+
+    load("y", "xt", 512, T.x[:, :], "lx")
+    load("s", "rlt", 32, T.rt[:, 0:32], "lrt", 512)
+    load("s", "gt", 512, T.gr[:, :], "lgr")
+    load("y", "wb", 2048, T.w[:, :], "lw")
+    load("s", "pb", 4, T.pr[:, 0:4], "lpr")
+    load("s", "ubb", 2048, T.ub[:, :], "lub")
+    load("y", "vb", 512, T.v[:, :], "lv")
+
+    iota("pi", 1, [[1, 1]], cm=1)
+    iota("ti", 128, [[1, 128]])
+    iota("rp", 128, [[0, 8], [1, 16]])
+    iota("bi", 3, [[16, 3]])
+    iota("em16", 16, [[1, 8], [0, 2]])
+    iota("g48", 48, [[1, 8], [100, 2], [0, 3]])
+    iota("e128", 128, [[1, 8], [0, 16]])
+    iota("fx", 24, [[16, 3], [96, 8]])
+    iota("si8", 8, [[1, 8]])
+    iota("s96", 96, [[16, 3], [0, 2], [1, 16]])
+    iota("h96", 96, [[0, 3], [1, 2], [0, 16]])
+    iota("cp16", 16, [[20, 2], [1, 8]])
+    col = lambda k: R("sc", k, k + 1)
+    pF, iF, eF, hF, e100, eh, qsel, z16 = [col(k) for k in range(8)]
+    TI, RP, E128 = R("ti", 0, 128), R("rp", 0, 128), R("e128", 0, 128)
+    for lane in (2, 3):
+        ms(R("rlt", lane, 512, 4), 0.0)
+        ms(R("rlt", 544 + lane, 1056, 4), 0.0)
+    p0 = R("pi", 0, 1)
+    ts(R("pi", 1, 2), p0, 15, None, A.bitwise_and)
+    ts(R("pi", 2, 3), p0, 4, None, A.arith_shift_right)
+    ts(R("pi", 3, 4), p0, 4, 1, A.arith_shift_right, A.bitwise_and)
+    cp(R("sc", 0, 4), R("pi", 0, 4))
+    ts(R("rlt", 0, 512, 4), TI, pF, None, A.is_ge)
+    act(R("rlt", 1, 512, 4), R("rlt", 0, 512, 4), F.Copy)
+    ts(R("rlt", 544, 1056, 4), TI, pF, None, A.is_equal)
+    ts(R("rlt", 545, 1056, 4), TI, pF, 2.0, A.is_equal, A.mult)
+    ts(R("rst", 0, 512, 4), RP, iF, None, A.is_equal)
+    for lane in (1, 2, 3):
+        act(R("rst", lane, 512, 4), R("rst", 0, 512, 4), F.Copy)
+    ms(R("xt", 512, 544), 0.0)
+    ms(R("gt", 512, 544), 0.0)
+    ms(R("pm", 0, 1), -9e29)
+    ms(R("pm2", 0, 1), -9e29)
+    ms(R("z8", 0, 8), 0.0)
+    qz("rlq", 128, 136, "rlt", 512)
+    for lane in (2, 3):
+        ms(R("tk", lane, 512, 4), 0.0)
+    qz("rlq", 0, 128, "rlt", 0)
+    ts(R("bib", 0, 3), R("bi", 0, 3), iF, 0.5, A.add, A.add)
+    ts(R("emv", 0, 16), R("em16", 0, 16), eF, None, A.is_equal)
+    ms(R("bt", 192, 512), 0.0)
+    ts(e100, eF, 100.0, None, A.add)
+    ts(R("bt", 2, 192, 4), R("g48", 0, 48), e100, 256.0, A.is_equal, A.mult)
+    ts(R("bt", 3, 192, 4), R("g48", 0, 48), e100, 16.0, A.is_equal, A.mult)
+    qz("xq", 0, 136, "xt")
+    mm("ps0", "xq", 0, "rlq", 128, 128)
+    qz("rq", 0, 128, "rst")
+
+    S = R("ps0", 0, 8)
+    scan(R("pm", 1, 9), S, R("z8", 0, 8))
+    act(R("junk", 0, 8), R("pm", 1, 9), F.Sign, -1.0, R("pm", 8, 9), R("iab", 0, 1))
+    ts(R("cm", 0, 9), R("pm", 0, 9), R("pm", 8, 9), BIG, A.is_equal, A.mult)
+    tt(R("ab", 0, 8), R("cm", 1, 9), R("cm", 0, 8), A.subtract)
+    tt(R("s2", 0, 8), S, R("ab", 0, 8), A.subtract)
+    scan(R("pm2", 1, 9), R("s2", 0, 8), R("z8", 0, 8))
+    act(R("junk", 8, 16), R("pm2", 1, 9), F.Sign, -1.0, R("pm2", 8, 9), R("iab", 1, 2))
+    ts(R("tk", 0, 512, 4), E128, R("iab", 0, 1), None, A.is_equal)
+    ts(R("tk", 1, 512, 4), E128, R("iab", 1, 2), None, A.is_equal)
+    qz("tkq", 0, 128, "tk")
+
+    mm("ps1", "tkq", 0, "rlq", 0, 130)
+    mm("ps2", "tkq", 0, "rlq", 0, 130)
+    mm("ps3", "tkq", 0, "rlq", 134, 130)
+    for k in range(2):
+        act(R("junk", 16 + 128 * k, 144 + 128 * k), R("ps1", 0, 128), F.Sign, -1.0, R("bib", k, k + 1), R("acc", k, k + 1))
+    qz("xq", 136, 136, "gt")
+    ts(R("tmpc", 0, 128), R("ps2", 0, 128), R("bib", 2, 3), 0.5, A.is_lt, A.subtract)
+    red(R("acc", 2, 3), R("tmpc", 0, 128), A.add)
+    ts(R("n48", 2, 48, 3), R("emv", 0, 16), R("acc", 2, 3), 2.0, A.mult, A.mult)
+    for k in range(2):
+        ts(R("n48", k, 48, 3), R("emv", 0, 16), R("acc", k, k + 1), None, A.mult)
+    ts(R("bt", 0, 192, 4), R("n48", 0, 48), MAGIC16, MAGIC16, A.add, A.subtract)
+    tt(R("bt", 1, 192, 4), R("n48", 0, 48), R("bt", 0, 192, 4), A.subtract)
+    qz("xq", 272, 128, "bt")
+    mm("ps4", "rq", 0, "xq", 262, 128)
+    ts(R("off", 0, 48), R("ps4", 10, 58), 0.5, 64.0, A.mult, A.add)
+    pick("sl", 0, 768, "xq", 272, "off", 0)
+
+    send("sl", 96, 96, "ld", 96, "arc", True)
+    send("sl_s", 96, 96, "ld_s", 96, "arp", False)
+    localcopy("sl", 96 * q, "ld", 96 * q, 96, "owc", True)
+    localcopy("sl_s", 96 * q, "ld_s", 96 * q, 96, "owp", False)
+    arrives("ld", 96, "arc")
+    arrives("ld_s", 96, "arp")
+
+    ms(R("ebt", 0, 2048), 0.0)
+    for b in range(4):
+        act(R("ebt", 513 * b, 512 * b + 512, 4), R("rlt", 544, 1056, 4), F.Copy)
+    act(R("wt", 0, 128), R("ps3", 2, 130), F.Copy)
+    qz("wq", 0, 512, "wb")
+    ts(R("ofx", 0, 24), R("fx", 0, 24), iF, None, A.add)
+    ts(R("ofg", 0, 24), R("fx", 0, 24), iF, 48.0, A.add, A.add)
+    qz("ebq", 0, 512, "ebt")
+    ms(R("ones", 0, 128), 1.0)
+    for b in range(4):
+        ts(R("prt", b, 512, 4), R("ones", 0, 128), R("pb", b, b + 1), None, A.mult)
+    qz("prq", 0, 128, "prt")
+    ts(R("o96", 0, 96), R("h96", 0, 96), hF, -BIG, A.not_equal, A.mult)
+    ts(R("sc", 9, 12), R("bib", 0, 3), 0.5, None, A.subtract)
+    for k in range(3):
+        c = R("cc", 96 * k, 96 * k + 96)
+        ts(c, R("s96", 0, 96), col(9 + k), TINY, A.is_lt, A.mult)
+        tt(c, c, R("o96", 0, 96), A.add)
+    ms(R("at", 3, 512, 4), 1.0)
+    for lane in (1, 2):
+        ms(R("at", 512 + lane, 528, 4), 0.0)
+    ts(R("sc", 12, 13), pF, float(q), 64.0, A.not_equal, A.mult)
+    ts(R("at", 515, 528, 4), R("ones", 0, 4), R("sc", 12, 13), None, A.mult)
+    ms(R("rk", 3, 4), 0.0)
+    ms(R("blt", 0, 544), 0.0)
+    SI = R("si8", 0, 8)
+    for k in (1, 2):
+        ts(R("blt", k, 32, 4), SI, eF, 128.0 * k, A.is_equal, A.mult)
+    ts(z16, pF, 0.0, 16.0, A.is_equal, A.mult)
+    ts(R("blt", 3, 32, 4), SI, z16, None, A.mult)
+    for k in range(3):
+        ts(R("blt", 32 + k, 64, 4), SI, eF, iF, A.is_equal, A.mult)
+    qz("blq", 0, 136, "blt")
+    ts(R("pi", 1, 2), p0, 3, None, A.bitwise_and)
+    ts(R("sc", 13, 14), R("pi", 1, 2), 512.0, None, A.add)
+    ts(R("of2", 1, 16, 2), R("ones", 0, 8), R("sc", 13, 14), None, A.mult)
+    qz("uq", 0, 512, "ubb")
+    qz("vq", 0, 128, "vb")
+
+    pick("xe", 0, 384, "ld", 768, "ofx", 0)
+    pick("ge", 0, 384, "ld", 768, "ofg", 0)
+    for i in range(4):
+        mm("ps%d" % i, "wq", 128 * i, "xe", 0, 384)
+    for b in range(4):
+        mm("ps%d" % (4 + b), "ebq", 128 * b, "ge", 0, 384)
+    MK = lambda b: R("mk", 384 * b, 384 * b + 384)
+    for b in (0, 2):
+        ts(MK(b), R("ps%d" % b, 0, 384), 0.0, None, A.is_gt)
+    for n, b in enumerate((1, 3)):
+        act(R("sg", 384 * n, 384 * n + 384), R("ps%d" % b, 0, 384), F.Sign)
+        act(MK(b), R("sg", 384 * n, 384 * n + 384), F.Relu)
+    for b in range(4):
+        tt(R("mt", b, 1536, 4), R("ps%d" % (4 + b), 0, 384), MK(b), A.mult)
+    for k in range(3):
+        qz("mq", 128 * k, 128, "mt", 512 * k)
+
+    for k in range(3):
+        mm("ps%d" % k, "mq", 128 * k, "prq", 0, 128)
+    for i in range(4):
+        mm("ps%d" % (4 + i), "uq", 128 * i, "mq", 0, 384)
+    for k in range(3):
+        act(R("ys", 32 * k, 32 * k + 32), R("ps%d" % k, 0, 32), F.Abs)
+    op("v", [R("ys", 0, 96)], [R("t96", 0, 96)], lambda: g.vector.transpose(T.t96[:, 0:96], T.ys[:, 0:96]))
+    T96 = R("t96", 0, 96)
+    D = lambda k: R("dd", 96 * k, 96 * k + 96)
+    C = lambda k: R("cmp", 96 * k, 96 * k + 96)
+    st = lambda k: R("ys", 32 * k, 32 * k + 1)
+    rk = lambda k: R("rk", k, k + 1)
+    for k in (1, 2):
+        act(D(k), T96, F.Identity, -1.0, st(k))
+    ts(D(0), T96, st(0), -1.0, A.subtract, A.mult)
+    for k in range(3):
+        tt(C(k), D(k), R("cc", 96 * k, 96 * k + 96), A.is_lt)
+    for k in (0, 1):
+        act(R("junk", 96 * k, 96 * k + 96), C(k), F.Copy, acc=rk(k))
+    red(rk(2), C(2), A.add)
+    for k in (0, 1, 2):
+        ts(R("at", k, 512, 4), RP, rk(k), None, A.is_equal)
+    cp(R("at", 512, 528, 4), R("rk", 0, 4))
+    qz("dxw", 384, 132, "at")
+    mm("ps3", "dxw", 384, "blq", 0, 128, True, False)
+    mm("ps3", "dxw", 384, "blq", 8, 128, False, True)
+    for i in range(3):
+        act(R("dxt", i, 1536, 4), R("ps%d" % (4 + i), 0, 384), F.Copy, 0.0625)
+    ts(R("dxt", 3, 1536, 4), R("ps7", 0, 384), 0.0625, None, A.mult)
+    cp(R("of2", 0, 16, 2), R("ps3", 0, 8))
+    qz("dxw", 0, 384, "dxt")
+    pick("ret", 0, 256, "dxw", 516, "of2", 0)
+
+    send("ret", 32, 20, "rl", 20, "rec", True)
+    send("ret_s", 32, 20, "rl_s", 20, "rep", False)
+    localcopy("ret", 32 * q, "rl", 20 * q, 20, "orc", True)
+    localcopy("ret_s", 32 * q, "rl_s", 20 * q, 20, "orp", False)
+    arrives("rl", 20, "rec")
+    arrives("rl_s", 20, "rep")
+
+    k3 = lambda n: R(n, 0, 3)
+    ms(R("kt", 1, 512, 4), 0.0)
+    ms(R("kt", 2, 512, 4), 0.0)
+    ts(qsel, eF, float(q), None, A.is_equal)
+    ts(R("kt", 0, 512, 4), RP, iF, qsel, A.is_equal, A.mult)
+    ts(R("kt", 3, 512, 4), E128, pF, None, A.is_equal)
+    qz("kq", 0, 128, "kt")
+    ts(R("tok", 0, 2), R("acc", 0, 2), 0.5, 64.0, A.mult, A.add)
+    ts(R("tok", 2, 3), R("acc", 2, 3), 64.0, None, A.add)
+    ts(k3("mm_"), k3("tok"), 7.5, 0.0625, A.subtract, A.mult)
+    ms(R("oht", 3, 512, 4), 0.0)
+    ts(k3("mm_"), k3("mm_"), MAGIC1, MAGIC1, A.add, A.subtract)
+    for k in range(3):
+        ts(R("oh", 128 * k, 128 * k + 128), TI, R("tok", k, k + 1), None, A.is_equal)
+    for k in range(3):
+        tt(R("oht", k, 512, 4), R("oh", 128 * k, 128 * k + 128), R("wt", 0, 128), A.mult)
+        act(R("junk", 128 * k, 128 * k + 128), R("oht", k, 512, 4), F.Copy, acc=R("wk", k, k + 1))
+    ts(k3("rr_"), k3("mm_"), -16.0, None, A.mult)
+    tt(k3("rr_"), k3("rr_"), k3("tok"), A.add)
+    for k in range(3):
+        ts(R("aht", k, 512, 4), RP, R("rr_", k, k + 1), 20.0, A.is_equal, A.mult)
+        ts(R("aht", 512 + k, 1024, 4), RP, R("rr_", k, k + 1), None, A.is_equal)
+    ms(R("aht", 3, 1024, 4), 0.0)
+    qz("ahq", 0, 256, "aht")
+    ts(k3("cd"), k3("wk"), 20.0, -20.0, A.mult, A.add)
+    tt(k3("cd"), k3("cd"), k3("mm_"), A.add)
+    ts(eh, eF, 8.0, None, A.subtract)
+    for k in range(3):
+        ts(R("mka", 16 * k, 16 * k + 16), R("cp16", 0, 16), R("cd", k, k + 1), None, A.is_equal)
+        ts(R("mkh", 16 * k, 16 * k + 16), R("cp16", 0, 16), R("cd", k, k + 1), eh, A.is_equal, A.mult)
+    ms(R("zer", 0, 512), 0.0)
+    qz("rl", 160, 128, "zer")
+    ms(R("bt2", 0, 640), 0.0)
+    qz("ohq", 0, 128, "oht")
+
+    mm("ps0", "kq", 0, "rl", 0, 160)
+    for k in range(3):
+        red(R("rkh", k, k + 1), R("ps0", 16 + k, 160, 20), A.min)
+    ts(k3("rth"), k3("rkh"), 15.5, None, A.is_lt)
+    for k in range(3):
+        act(R("bt2", k, 64, 4), R("mkh", 16 * k, 16 * k + 16), F.Copy, R("rth", k, k + 1))
+    tt(k3("rrh"), k3("rkh"), k3("rth"), A.mult)
+    cp(R("bt2", 128, 131), k3("rth"))
+    for k in range(3):
+        ts(R("bt2", 64 + k, 128, 4), R("mka", 16 * k, 16 * k + 16), R("rrh", k, k + 1), None, A.mult)
+    qz("btq", 0, 160, "bt2")
+    mm("ps1", "ahq", 0, "btq", 0, 128, True, False)
+    mm("ps1", "ahq", 128, "btq", 16, 128, False, True)
+    mm("ps2", "btq", 32, "ohq", 0, 128)
+    ts(R("of3", 0, 16), R("ps1", 0, 16), 160.0, None, A.add)
+    pick("zc", 0, 256, "rl", 162, "of3", 0)
+    act(R("ctsb", 0, 128), R("ps2", 0, 128), F.Copy)
+    dma("y", [R("ctsb", 0, 128)], [], T.ct[:, :], T.ctsb[0:1, 0:128], "o_ct")
+    for b in range(4):
+        mm("ps%d" % (4 + b), "ebq", 128 * b, "zc", 0, 128, True, False)
+        mm("ps%d" % (4 + b), "ebq", 128 * b, "zc", 128, 128, False, True)
+    for b in (0, 2):
+        act(R("zt", b, 512, 4), R("ps%d" % (4 + b), 0, 128), F.Copy)
+    for b in (1, 3):
+        cp(R("zt", b, 512, 4), R("ps%d" % (4 + b), 0, 128))
+    qz("zq", 0, 128, "zt")
+    mm("ps3", "vq", 0, "zq", 0, 128)
+    dma("y", [R("zq", 0, 128)], [], T.oc[:, :], T.zq[:, 0:128].bitcast(dt.uint8), "o_oc")
+    for k in range(4):
+        dma("y" if k < 1 else "s", [R("zq_s", 0, 128)], [], T.osc[4 * k:4 * k + 4, 0:128], T.zq_s[32 * k:32 * k + 4, 0:128], "o_s%d" % k)
+    cp(R("ysb", 0, 128), R("ps3", 0, 128))
+    dma("y", [R("ysb", 0, 128)], [], T.y[:, :], T.ysb[:, 0:128], "o_y")
+
+    for s, v in total.items():
+        wait("g", s, v)

@@ -23,11 +23,11 @@ for _n, _w in (("xq", 400), ("rlq", 264), ("tkq", 128), ("rq", 128), ("sl", 768)
                ("kq", 128), ("ahq", 256), ("ohq", 128), ("btq", 160), ("zc", 256), ("zq", 128)):
     _mx(_n, _w)
 for _n, _w in (("xt", 544), ("gt", 544), ("rlt", 1056), ("tk", 512), ("bt", 512), ("rst", 512), ("wb", 2048), ("ubb", 2048), ("vb", 512),
-               ("pb", 4), ("prt", 512), ("ebt", 2048), ("mt", 1536), ("dxt", 1536), ("blt", 544), ("at", 528), ("kt", 512), ("aht", 1024),
+               ("pb", 4), ("prt", 512), ("eye", 520), ("mt", 1536), ("dxt", 1536), ("blt", 544), ("at", 528), ("kt", 512), ("aht", 1024),
                ("oht", 512), ("bt2", 640), ("zt", 512), ("zer", 512), ("ones", 128), ("ti", 128), ("e128", 128), ("rp", 128), ("tmpc", 128),
                ("wt", 128), ("oh", 384), ("mk", 1536), ("sg", 768), ("junk", 384), ("mka", 48), ("mkh", 48)):
     _sb(_n, _w, "bfloat16")
-for _n, _w in (("sc", 16), ("cc", 288), ("pm", 16), ("pm2", 16), ("cm", 16), ("ab", 8), ("s2", 8), ("iab", 4),
+for _n, _w in (("sc", 32), ("cc", 288), ("pm", 16), ("pm2", 16), ("cm", 16), ("ab", 8), ("s2", 8), ("iab", 4),
                ("acc", 4), ("n48", 48), ("ys", 96), ("t96", 96), ("dd", 288), ("cmp", 288), ("rk", 4), ("tok", 4), ("mm_", 4), ("rr_", 4),
                ("wk", 4), ("cd", 4), ("rkh", 4), ("rth", 4), ("rrh", 4), ("ysb", 128), ("ctsb", 128)):
     _sb(_n, _w)
@@ -176,19 +176,19 @@ def rank_program(g, core, T, topo):
             e = topo.engines(core, c)[first::2]
             masks[c] = (1 << e[2 * j]) | (1 << e[2 * j + 1])
 
-    def send(src, sw, width, dst, dw, s, code):
-        depend("g", [R(src, 0, sw * N)], [])
+    def send(src, sw, at, width, dst, dw, s, code, to):
+        blocks = [R(src, sw * T.rank_of(c) + at, sw * T.rank_of(c) + at + width) for c in to]
+        depend("g", blocks, [])
         ts_ = []
-        for c in peers:
-            e = T.rank_of(c)
+        for c, r in zip(to, blocks):
             rid, pid = topo.addr(c)[:2]
-            a, b = T[src][:, sw * e:sw * e + width], T[dst][:, dw * q:dw * q + width]
+            a, b = ap(r), T[dst][:, dw * q:dw * q + width]
             if code:
                 a, b = a.bitcast(dt.uint8), b.bitcast(dt.uint8)
             ts_.append(RemoteDMATransfer(dst_ids=[DstId(rid=rid, pnc=pid)], dma_engine_mask=masks[c], remote_sem=T.sem[s], src=a, dst=b))
         g.remote_dma_fused(ts_, local_sem=T.sem["loc"])
-        total["loc"] = total.get("loc", 0) + 2 * len(peers)
-        note("dma", [R(src, 0, sw * N)], [], "loc", total["loc"])
+        total["loc"] = total.get("loc", 0) + 2 * len(to)
+        note("dma", blocks, [], "loc", total["loc"])
 
     def arrives(dst, dw, s):
         total[s] = 2 * len(peers)
@@ -207,9 +207,9 @@ def rank_program(g, core, T, topo):
 
     load("y", "xt", 512, T.x[:, :], "lx")
     load("s", "rlt", 32, T.rt[:, 0:32], "lrt", 512)
-    load("s", "gt", 512, T.gr[:, :], "lgr")
-    load("y", "wb", 2048, T.w[:, :], "lw")
+    load("y", "gt", 512, T.gr[:, :], "lgr")
     load("s", "pb", 4, T.pr[:, 0:4], "lpr")
+    load("y", "wb", 2048, T.w[:, :], "lw")
     load("s", "ubb", 2048, T.ub[:, :], "lub")
     load("y", "vb", 512, T.v[:, :], "lv")
 
@@ -222,9 +222,7 @@ def rank_program(g, core, T, topo):
     iota("e128", 128, [[1, 8], [0, 16]])
     iota("fx", 24, [[16, 3], [96, 8]])
     iota("si8", 8, [[1, 8]])
-    iota("s96", 96, [[16, 3], [0, 2], [1, 16]])
-    iota("h96", 96, [[0, 3], [1, 2], [0, 16]])
-    iota("cp16", 16, [[20, 2], [1, 8]])
+    iota("eye", 520, [[0, 520]])
     col = lambda k: R("sc", k, k + 1)
     pF, iF, eF, hF, e100, eh, qsel, z16 = [col(k) for k in range(8)]
     TI, RP, E128 = R("ti", 0, 128), R("rp", 0, 128), R("e128", 0, 128)
@@ -248,7 +246,6 @@ def rank_program(g, core, T, topo):
     ms(R("pm", 0, 1), -9e29)
     ms(R("pm2", 0, 1), -9e29)
     ms(R("z8", 0, 8), 0.0)
-    qz("rlq", 128, 136, "rlt", 512)
     for lane in (2, 3):
         ms(R("tk", lane, 512, 4), 0.0)
     qz("rlq", 0, 128, "rlt", 0)
@@ -258,9 +255,10 @@ def rank_program(g, core, T, topo):
     ts(e100, eF, 100.0, None, A.add)
     ts(R("bt", 2, 192, 4), R("g48", 0, 48), e100, 256.0, A.is_equal, A.mult)
     ts(R("bt", 3, 192, 4), R("g48", 0, 48), e100, 16.0, A.is_equal, A.mult)
-    qz("xq", 0, 136, "xt")
-    mm("ps0", "xq", 0, "rlq", 128, 128)
     qz("rq", 0, 128, "rst")
+    qz("xq", 0, 136, "xt")
+    qz("rlq", 128, 136, "rlt", 512)
+    mm("ps0", "xq", 0, "rlq", 128, 128)
 
     S = R("ps0", 0, 8)
     scan(R("pm", 1, 9), S, R("z8", 0, 8))
@@ -282,41 +280,54 @@ def rank_program(g, core, T, topo):
     qz("xq", 136, 136, "gt")
     ts(R("tmpc", 0, 128), R("ps2", 0, 128), R("bib", 2, 3), 0.5, A.is_lt, A.subtract)
     red(R("acc", 2, 3), R("tmpc", 0, 128), A.add)
-    ts(R("n48", 2, 48, 3), R("emv", 0, 16), R("acc", 2, 3), 2.0, A.mult, A.mult)
     for k in range(2):
         ts(R("n48", k, 48, 3), R("emv", 0, 16), R("acc", k, k + 1), None, A.mult)
+    ts(R("n48", 2, 48, 3), R("emv", 0, 16), R("acc", 2, 3), 2.0, A.mult, A.mult)
     ts(R("bt", 0, 192, 4), R("n48", 0, 48), MAGIC16, MAGIC16, A.add, A.subtract)
     tt(R("bt", 1, 192, 4), R("n48", 0, 48), R("bt", 0, 192, 4), A.subtract)
     qz("xq", 272, 128, "bt")
     mm("ps4", "rq", 0, "xq", 262, 128)
     ts(R("off", 0, 48), R("ps4", 10, 58), 0.5, 64.0, A.mult, A.add)
-    pick("sl", 0, 768, "xq", 272, "off", 0)
 
-    send("sl", 96, 96, "ld", 96, "arc", True)
-    send("sl_s", 96, 96, "ld_s", 96, "arp", False)
+    there = [T.rank_of(c) for c in far]
+    for group in (there, [e for e in range(N) if e not in there]):
+        for e in group:
+            if e - 1 not in group:
+                n = 1
+                while e + n in group:
+                    n += 1
+                pick("sl", 96 * e, 96 * n, "xq", 272, "off", 6 * e)
+    send("sl", 96, 0, 96, "ld", 96, "arc", True, far)
+    send("sl", 96, 0, 96, "ld", 96, "arc", True, near)
+    send("sl_s", 96, 0, 96, "ld_s", 96, "arp", False, peers)
     localcopy("sl", 96 * q, "ld", 96 * q, 96, "owc", True)
     localcopy("sl_s", 96 * q, "ld_s", 96 * q, 96, "owp", False)
     arrives("ld", 96, "arc")
     arrives("ld_s", 96, "arp")
 
-    ms(R("ebt", 0, 2048), 0.0)
-    for b in range(4):
-        act(R("ebt", 513 * b, 512 * b + 512, 4), R("rlt", 544, 1056, 4), F.Copy)
+    iota("s96", 96, [[16, 3], [0, 2], [1, 16]])
+    iota("h96", 96, [[0, 3], [1, 2], [0, 16]])
+    iota("cp16", 16, [[20, 2], [1, 8]])
+    iota("zer", 512, [[0, 512]])
+    iota("bt2", 640, [[0, 640]])
     act(R("wt", 0, 128), R("ps3", 2, 130), F.Copy)
+    ts(R("eye", 4, 516, 4), TI, pF, None, A.is_equal)
+    ms(R("ones", 0, 128), 1.0)
+    cp(R("sc", 16, 20), R("pb", 0, 4))
+    for b in range(4):
+        act(R("prt", b, 512, 4), R("ones", 0, 128), F.Copy, col(16 + b))
+    for b in range(4):
+        qz("ebq", 128 * b, 128, "eye", 4 - b)
     qz("wq", 0, 512, "wb")
     ts(R("ofx", 0, 24), R("fx", 0, 24), iF, None, A.add)
     ts(R("ofg", 0, 24), R("fx", 0, 24), iF, 48.0, A.add, A.add)
-    qz("ebq", 0, 512, "ebt")
-    ms(R("ones", 0, 128), 1.0)
-    for b in range(4):
-        ts(R("prt", b, 512, 4), R("ones", 0, 128), R("pb", b, b + 1), None, A.mult)
     qz("prq", 0, 128, "prt")
     ts(R("o96", 0, 96), R("h96", 0, 96), hF, -BIG, A.not_equal, A.mult)
-    ts(R("sc", 9, 12), R("bib", 0, 3), 0.5, None, A.subtract)
+    ts(R("s96", 0, 96), R("s96", 0, 96), -TINY, None, A.mult)
+    ts(R("sc", 9, 12), R("bib", 0, 3), 0.5, TINY, A.subtract, A.mult)
+    tt(R("o96", 0, 96), R("o96", 0, 96), R("s96", 0, 96), A.add)
     for k in range(3):
-        c = R("cc", 96 * k, 96 * k + 96)
-        ts(c, R("s96", 0, 96), col(9 + k), TINY, A.is_lt, A.mult)
-        tt(c, c, R("o96", 0, 96), A.add)
+        ts(R("cc", 96 * k, 96 * k + 96), R("o96", 0, 96), col(9 + k), None, A.add)
     ms(R("at", 3, 512, 4), 1.0)
     for lane in (1, 2):
         ms(R("at", 512 + lane, 528, 4), 0.0)
@@ -334,33 +345,53 @@ def rank_program(g, core, T, topo):
     qz("blq", 0, 136, "blt")
     ts(R("pi", 1, 2), p0, 3, None, A.bitwise_and)
     ts(R("sc", 13, 14), R("pi", 1, 2), 512.0, None, A.add)
-    ts(R("of2", 1, 16, 2), R("ones", 0, 8), R("sc", 13, 14), None, A.mult)
+    ts(R("of2", 0, 16, 2), R("ones", 0, 8), R("sc", 13, 14), None, A.mult)
     qz("uq", 0, 512, "ubb")
     qz("vq", 0, 128, "vb")
 
-    pick("xe", 0, 384, "ld", 768, "ofx", 0)
-    pick("ge", 0, 384, "ld", 768, "ofg", 0)
-    for i in range(4):
-        mm("ps%d" % i, "wq", 128 * i, "xe", 0, 384)
-    for b in range(4):
-        mm("ps%d" % (4 + b), "ebq", 128 * b, "ge", 0, 384)
-    MK = lambda b: R("mk", 384 * b, 384 * b + 384)
-    for b in (0, 2):
-        ts(MK(b), R("ps%d" % b, 0, 384), 0.0, None, A.is_gt)
-    for n, b in enumerate((1, 3)):
-        act(R("sg", 384 * n, 384 * n + 384), R("ps%d" % b, 0, 384), F.Sign)
-        act(MK(b), R("sg", 384 * n, 384 * n + 384), F.Relu)
-    for b in range(4):
-        tt(R("mt", b, 1536, 4), R("ps%d" % (4 + b), 0, 384), MK(b), A.mult)
-    for k in range(3):
-        qz("mq", 128 * k, 128, "mt", 512 * k)
+    MK = lambda b, o: R("mk", 384 * b + o, 384 * b + o + 128)
+
+    def arrange(o):
+        pick("xe", o, 128, "ld", 768, "ofx", o // 16)
+        pick("ge", o, 128, "ld", 768, "ofg", o // 16)
+
+    arrange(0)
+    for o in (0, 128, 256):
+        for i in range(4):
+            mm("ps%d" % i, "wq", 128 * i, "xe", o, 128)
+        if o < 256:
+            arrange(o + 128)
+        for b in range(4):
+            mm("ps%d" % (4 + b), "ebq", 128 * b, "ge", o, 128)
+        for b in (0, 2):
+            ts(MK(b, o), R("ps%d" % b, 0, 128), 0.0, None, A.is_gt)
+        for j, b in enumerate((1, 3)):
+            act(R("sg", 384 * j + o, 384 * j + o + 128), R("ps%d" % b, 0, 128), F.Sign)
+            act(MK(b, o), R("sg", 384 * j + o, 384 * j + o + 128), F.Relu)
+        for b in range(4):
+            tt(R("mt", 4 * o + b, 4 * o + 512, 4), R("ps%d" % (4 + b), 0, 128), MK(b, o), A.mult)
+        qz("mq", o, 128, "mt", 4 * o)
+
+    parts = ((0, 256), (256, 128))
+    UB = lambda h, i: "ps%d" % (4 - 4 * h + i)
+
+    def products(h):
+        for i in range(4):
+            mm(UB(h, i), "uq", 128 * i, "mq", parts[h][0], parts[h][1])
+
+    def shrink(h, i):
+        o, n = parts[h]
+        if i < 3:
+            act(R("dxt", 4 * o + i, 4 * (o + n), 4), R(UB(h, i), 0, n), F.Copy, 0.0625)
+        else:
+            ts(R("dxt", 4 * o + i, 4 * (o + n), 4), R(UB(h, i), 0, n), 0.0625, None, A.mult)
 
     for k in range(3):
         mm("ps%d" % k, "mq", 128 * k, "prq", 0, 128)
-    for i in range(4):
-        mm("ps%d" % (4 + i), "uq", 128 * i, "mq", 0, 384)
+    products(0)
     for k in range(3):
         act(R("ys", 32 * k, 32 * k + 32), R("ps%d" % k, 0, 32), F.Abs)
+    products(1)
     op("v", [R("ys", 0, 96)], [R("t96", 0, 96)], lambda: g.vector.transpose(T.t96[:, 0:96], T.ys[:, 0:96]))
     T96 = R("t96", 0, 96)
     D = lambda k: R("dd", 96 * k, 96 * k + 96)
@@ -372,6 +403,7 @@ def rank_program(g, core, T, topo):
     ts(D(0), T96, st(0), -1.0, A.subtract, A.mult)
     for k in range(3):
         tt(C(k), D(k), R("cc", 96 * k, 96 * k + 96), A.is_lt)
+    shrink(0, 0)
     for k in (0, 1):
         act(R("junk", 96 * k, 96 * k + 96), C(k), F.Copy, acc=rk(k))
     red(rk(2), C(2), A.add)
@@ -379,64 +411,64 @@ def rank_program(g, core, T, topo):
         ts(R("at", k, 512, 4), RP, rk(k), None, A.is_equal)
     cp(R("at", 512, 528, 4), R("rk", 0, 4))
     qz("dxw", 384, 132, "at")
-    mm("ps3", "dxw", 384, "blq", 0, 128, True, False)
-    mm("ps3", "dxw", 384, "blq", 8, 128, False, True)
-    for i in range(3):
-        act(R("dxt", i, 1536, 4), R("ps%d" % (4 + i), 0, 384), F.Copy, 0.0625)
-    ts(R("dxt", 3, 1536, 4), R("ps7", 0, 384), 0.0625, None, A.mult)
-    cp(R("of2", 0, 16, 2), R("ps3", 0, 8))
-    qz("dxw", 0, 384, "dxt")
+    for i in (1, 2, 3):
+        shrink(0, i)
+    qz("dxw", 0, 256, "dxt")
+    mm("ps4", "dxw", 384, "blq", 0, 128, True, False)
+    mm("ps4", "dxw", 384, "blq", 8, 128, False, True)
+    for i in range(4):
+        shrink(1, i)
+    qz("dxw", 256, 128, "dxt", 1024)
+    cp(R("of2", 1, 16, 2), R("ps4", 0, 8))
     pick("ret", 0, 256, "dxw", 516, "of2", 0)
 
-    send("ret", 32, 20, "rl", 20, "rec", True)
-    send("ret_s", 32, 20, "rl_s", 20, "rep", False)
-    localcopy("ret", 32 * q, "rl", 20 * q, 20, "orc", True)
-    localcopy("ret_s", 32 * q, "rl_s", 20 * q, 20, "orp", False)
+    send("ret", 32, 12, 20, "rl", 20, "rec", True, peers)
+    send("ret_s", 32, 12, 20, "rl_s", 20, "rep", False, peers)
+    localcopy("ret", 32 * q + 12, "rl", 20 * q, 20, "orc", True)
+    localcopy("ret_s", 32 * q + 12, "rl_s", 20 * q, 20, "orp", False)
     arrives("rl", 20, "rec")
     arrives("rl_s", 20, "rep")
 
     k3 = lambda n: R(n, 0, 3)
-    ms(R("kt", 1, 512, 4), 0.0)
-    ms(R("kt", 2, 512, 4), 0.0)
-    ts(qsel, eF, float(q), None, A.is_equal)
-    ts(R("kt", 0, 512, 4), RP, iF, qsel, A.is_equal, A.mult)
-    ts(R("kt", 3, 512, 4), E128, pF, None, A.is_equal)
-    qz("kq", 0, 128, "kt")
     ts(R("tok", 0, 2), R("acc", 0, 2), 0.5, 64.0, A.mult, A.add)
     ts(R("tok", 2, 3), R("acc", 2, 3), 64.0, None, A.add)
-    ts(k3("mm_"), k3("tok"), 7.5, 0.0625, A.subtract, A.mult)
     ms(R("oht", 3, 512, 4), 0.0)
-    ts(k3("mm_"), k3("mm_"), MAGIC1, MAGIC1, A.add, A.subtract)
+    ts(k3("mm_"), k3("tok"), 7.5, 0.0625, A.subtract, A.mult)
     for k in range(3):
         ts(R("oh", 128 * k, 128 * k + 128), TI, R("tok", k, k + 1), None, A.is_equal)
+    ts(k3("mm_"), k3("mm_"), MAGIC1, MAGIC1, A.add, A.subtract)
     for k in range(3):
         tt(R("oht", k, 512, 4), R("oh", 128 * k, 128 * k + 128), R("wt", 0, 128), A.mult)
         act(R("junk", 128 * k, 128 * k + 128), R("oht", k, 512, 4), F.Copy, acc=R("wk", k, k + 1))
     ts(k3("rr_"), k3("mm_"), -16.0, None, A.mult)
-    tt(k3("rr_"), k3("rr_"), k3("tok"), A.add)
-    for k in range(3):
-        ts(R("aht", k, 512, 4), RP, R("rr_", k, k + 1), 20.0, A.is_equal, A.mult)
-        ts(R("aht", 512 + k, 1024, 4), RP, R("rr_", k, k + 1), None, A.is_equal)
     ms(R("aht", 3, 1024, 4), 0.0)
-    qz("ahq", 0, 256, "aht")
+    tt(k3("rr_"), k3("rr_"), k3("tok"), A.add)
+    ts(qsel, eF, float(q), None, A.is_equal)
+    for k in range(3):
+        ts(R("aht", 512 + k, 1024, 4), RP, R("rr_", k, k + 1), None, A.is_equal)
+        act(R("aht", k, 512, 4), R("aht", 512 + k, 1024, 4), F.Copy, 20.0)
+    ts(R("kt", 0, 512, 4), RP, iF, qsel, A.is_equal, A.mult)
+    for lane in (1, 2):
+        ms(R("kt", lane, 512, 4), 0.0)
+    ts(R("kt", 3, 512, 4), E128, pF, None, A.is_equal)
+    qz("kq", 0, 128, "kt")
     ts(k3("cd"), k3("wk"), 20.0, -20.0, A.mult, A.add)
+    ts(eh, eF, 7.0, None, A.subtract)
     tt(k3("cd"), k3("cd"), k3("mm_"), A.add)
-    ts(eh, eF, 8.0, None, A.subtract)
+    qz("ahq", 0, 256, "aht")
     for k in range(3):
         ts(R("mka", 16 * k, 16 * k + 16), R("cp16", 0, 16), R("cd", k, k + 1), None, A.is_equal)
         ts(R("mkh", 16 * k, 16 * k + 16), R("cp16", 0, 16), R("cd", k, k + 1), eh, A.is_equal, A.mult)
-    ms(R("zer", 0, 512), 0.0)
     qz("rl", 160, 128, "zer")
-    ms(R("bt2", 0, 640), 0.0)
     qz("ohq", 0, 128, "oht")
 
     mm("ps0", "kq", 0, "rl", 0, 160)
     for k in range(3):
-        red(R("rkh", k, k + 1), R("ps0", 16 + k, 160, 20), A.min)
+        red(R("rkh", k, k + 1), R("ps0", k, 160, 20), A.min)
     ts(k3("rth"), k3("rkh"), 15.5, None, A.is_lt)
+    ts(k3("rrh"), k3("rkh"), 16.0, 16.0, A.min, A.subtract)
     for k in range(3):
         act(R("bt2", k, 64, 4), R("mkh", 16 * k, 16 * k + 16), F.Copy, R("rth", k, k + 1))
-    tt(k3("rrh"), k3("rkh"), k3("rth"), A.mult)
     cp(R("bt2", 128, 131), k3("rth"))
     for k in range(3):
         ts(R("bt2", 64 + k, 128, 4), R("mka", 16 * k, 16 * k + 16), R("rrh", k, k + 1), None, A.mult)
@@ -445,12 +477,12 @@ def rank_program(g, core, T, topo):
     mm("ps1", "ahq", 128, "btq", 16, 128, False, True)
     mm("ps2", "btq", 32, "ohq", 0, 128)
     ts(R("of3", 0, 16), R("ps1", 0, 16), 160.0, None, A.add)
-    pick("zc", 0, 256, "rl", 162, "of3", 0)
+    for h in range(2):
+        pick("zc", 128 * h, 128, "rl", 162, "of3", 8 * h)
+        for b in range(4):
+            mm("ps%d" % (4 + b), "ebq", 128 * b, "zc", 128 * h, 128, h == 0, h == 1)
     act(R("ctsb", 0, 128), R("ps2", 0, 128), F.Copy)
     dma("y", [R("ctsb", 0, 128)], [], T.ct[:, :], T.ctsb[0:1, 0:128], "o_ct")
-    for b in range(4):
-        mm("ps%d" % (4 + b), "ebq", 128 * b, "zc", 0, 128, True, False)
-        mm("ps%d" % (4 + b), "ebq", 128 * b, "zc", 128, 128, False, True)
     for b in (0, 2):
         act(R("zt", b, 512, 4), R("ps%d" % (4 + b), 0, 128), F.Copy)
     for b in (1, 3):

@@ -18,27 +18,27 @@ def _mx(name, n):
     _sb(name + "_s", n, "uint8")
 
 
-for _n, _w in (("xq", 400), ("rlq", 264), ("tkq", 128), ("rq", 128), ("sl", 768), ("ld", 768), ("xe", 384), ("ge", 384), ("wq", 512),
-               ("uq", 512), ("vq", 128), ("prq", 128), ("ebq", 512), ("mq", 384), ("dxw", 516), ("blq", 136), ("ret", 256), ("rl", 288),
-               ("kq", 128), ("ahq", 256), ("ohq", 128), ("btq", 160), ("zc", 256), ("zq", 128)):
+for _n, _w in (("xq", 400), ("rlq", 264), ("tkq", 128), ("rq", 128), ("sl", 768), ("ld", 768), ("xg", 768), ("wq", 512),
+               ("uq", 512), ("vq", 128), ("prq", 128), ("ebq", 512), ("mq", 384), ("dxw", 516), ("blq", 144), ("ret", 192), ("rl", 288),
+               ("kq", 128), ("ahq", 272), ("ohq", 128), ("btq", 128), ("ctq", 128), ("zc", 256), ("zq", 128)):
     _mx(_n, _w)
 for _n, _w in (("xt", 544), ("gt", 544), ("rlt", 1056), ("tk", 512), ("bt", 512), ("rst", 512), ("wb", 2048), ("ubb", 2048), ("vb", 512),
-               ("pb", 4), ("prt", 512), ("eye", 520), ("mt", 1536), ("dxt", 1536), ("blt", 544), ("at", 528), ("kt", 512), ("aht", 1024),
-               ("oht", 512), ("bt2", 640), ("zt", 512), ("zer", 512), ("ones", 128), ("ti", 128), ("e128", 128), ("rp", 128), ("tmpc", 128),
-               ("wt", 128), ("oh", 384), ("mk", 1536), ("sg", 768), ("junk", 384), ("mka", 48), ("mkh", 48)):
+               ("pb", 4), ("prt", 512), ("eye", 520), ("mt", 1536), ("dxt", 1536), ("blt", 576), ("at", 528), ("kt", 512), ("aht", 1088),
+               ("oht", 512), ("bt2", 512), ("zt", 512), ("zer", 512), ("ones", 128), ("ti", 128), ("e128", 128), ("rp", 128), ("tmpc", 128),
+               ("wt", 128), ("oh", 384), ("mk", 1536), ("sg", 768), ("junk", 384), ("mka", 48), ("dd", 288), ("cmp", 288), ("cc", 288)):
     _sb(_n, _w, "bfloat16")
-for _n, _w in (("sc", 32), ("cc", 288), ("pm", 16), ("pm2", 16), ("cm", 16), ("ab", 8), ("s2", 8), ("iab", 4),
-               ("acc", 4), ("n48", 48), ("ys", 96), ("t96", 96), ("dd", 288), ("cmp", 288), ("rk", 4), ("tok", 4), ("mm_", 4), ("rr_", 4),
-               ("wk", 4), ("cd", 4), ("rkh", 4), ("rth", 4), ("rrh", 4), ("ysb", 128), ("ctsb", 128)):
+for _n, _w in (("sc", 32), ("pm", 32), ("cm", 16), ("ab", 8), ("s2", 8), ("iab", 4), ("acc", 4), ("n48", 48), ("ys", 96), ("t96", 96),
+               ("rk", 4), ("tok", 4), ("mp", 4), ("mm_", 4), ("m16", 4), ("m20", 4), ("rr_", 4), ("wk", 4), ("w20", 4), ("cd", 4), ("rkh", 4),
+               ("ysb", 128), ("ctsb", 128)):
     _sb(_n, _w)
 _at = 0
-for _n, _w in (("em16", 16), ("emv", 16), ("g48", 48), ("bi", 16), ("bib", 16), ("si8", 16), ("cp16", 16), ("s96", 96), ("h96", 96),
-               ("o96", 96), ("fx", 32), ("z8", 16)):
+for _n, _w in (("em16", 16), ("emv", 16), ("g48", 48), ("bi", 16), ("bib", 16), ("d16", 16), ("cp16", 16), ("s96", 96), ("h96", 96),
+               ("o96", 96), ("fx", 48), ("z8", 16)):
     ALIAS[_n] = ("cs", _at)
     _at += _w
 _sb("cs", _at)
-_sb("pi", 4, "int32")
-for _n, _w in (("off", 48), ("ofx", 24), ("ofg", 24), ("of2", 16), ("of3", 16)):
+_sb("pi", 8, "int32")
+for _n, _w in (("off", 48), ("ofs", 48), ("of2", 16), ("of3", 16)):
     _sb(_n, _w, "uint16")
 for _k in range(8):
     SCRATCH["ps%d" % _k] = ("psum", [128, 512], "float32")
@@ -151,17 +151,27 @@ def rank_program(g, core, T, topo):
             op("s", rds(a, scale, bias), [out, acc],
                lambda: g.scalar.activation(ap(out), ap(a), f, bias=sc_(bias), scale=sc_(scale), accum_out=ap(acc)))
 
+    def zero(name, lane, hi=512, lo=0):
+        act(R(name, lo + lane, hi, 4), R("ti", 0, 128), F.Copy, 0.0)
+
     def mm(bank, lhs, l0, rhs, r0, n, start=True, stop=True):
         op("t", [R(lhs, l0, l0 + 128), R(lhs + "_s", l0, l0 + 128), R(rhs, r0, r0 + n), R(rhs + "_s", r0, r0 + n)], [R(bank, 0, n)],
            lambda: g.tensor.matmul_mx(T[bank][:, 0:n], T[lhs][:, l0:l0 + 128], T[lhs + "_s"][:, l0:l0 + 128],
                                       T[rhs][:, r0:r0 + n], T[rhs + "_s"][:, r0:r0 + n], start, stop))
 
-    def pick(out, o0, n, win, w1, off, f0):
+    def pickc(out, o0, n, win, w1, off, f0):
         fr = R(off, f0, f0 + n // 16)
         op("v", [R(win, 0, w1), fr], [R(out, o0, o0 + n)],
            lambda: g.vector.tensor_copy(T[out][:, o0:o0 + n].bitcast(dt.uint32), T[win][:, 0:w1].bitcast(dt.uint32).indirect(ap(fr))))
+
+    def picks(out, o0, n, win, w1, off, f0):
+        fr = R(off, f0, f0 + n // 16)
         op("s", [R(win + "_s", 0, w1), fr], [R(out + "_s", o0, o0 + n)],
            lambda: g.scalar.activation(T[out + "_s"][:, o0:o0 + n], T[win + "_s"][:, 0:w1].indirect(ap(fr)), F.Copy))
+
+    def pick(*a):
+        pickc(*a)
+        picks(*a)
 
     def iota(name, n, pattern, cm=0):
         r = R(name, 0, n)
@@ -176,13 +186,13 @@ def rank_program(g, core, T, topo):
             e = topo.engines(core, c)[first::2]
             masks[c] = (1 << e[2 * j]) | (1 << e[2 * j + 1])
 
-    def send(src, sw, at, width, dst, dw, s, code, to):
-        blocks = [R(src, sw * T.rank_of(c) + at, sw * T.rank_of(c) + at + width) for c in to]
+    def send(src, start, width, dst, s, code, to):
+        blocks = [R(src, start(T.rank_of(c)), start(T.rank_of(c)) + width) for c in to]
         depend("g", blocks, [])
         ts_ = []
         for c, r in zip(to, blocks):
             rid, pid = topo.addr(c)[:2]
-            a, b = ap(r), T[dst][:, dw * q:dw * q + width]
+            a, b = ap(r), T[dst][:, width * q:width * q + width]
             if code:
                 a, b = a.bitcast(dt.uint8), b.bitcast(dt.uint8)
             ts_.append(RemoteDMATransfer(dst_ids=[DstId(rid=rid, pnc=pid)], dma_engine_mask=masks[c], remote_sem=T.sem[s], src=a, dst=b))
@@ -216,49 +226,51 @@ def rank_program(g, core, T, topo):
     iota("pi", 1, [[1, 1]], cm=1)
     iota("ti", 128, [[1, 128]])
     iota("rp", 128, [[0, 8], [1, 16]])
-    iota("bi", 3, [[16, 3]])
     iota("em16", 16, [[1, 8], [0, 2]])
     iota("g48", 48, [[1, 8], [100, 2], [0, 3]])
+    iota("bi", 3, [[16, 3]])
+    iota("z8", 8, [[0, 8]])
     iota("e128", 128, [[1, 8], [0, 16]])
-    iota("fx", 24, [[16, 3], [96, 8]])
-    iota("si8", 8, [[1, 8]])
     iota("eye", 520, [[0, 520]])
+    iota("fx", 48, [[16, 3], [48, 2], [96, 8]])
+    iota("d16", 12, [[32, 4], [8, 3]])
+    iota("s96", 96, [[16, 3], [0, 2], [1, 16]])
+    iota("h96", 96, [[0, 3], [1, 2], [0, 16]])
     col = lambda k: R("sc", k, k + 1)
-    pF, iF, eF, hF, e100, eh, qsel, z16 = [col(k) for k in range(8)]
+    pF, iF, eF, hF, fF, e100, iH, flag, e16 = [col(k) for k in range(9)]
+    eh, qsel = col(12), col(13)
     TI, RP, E128 = R("ti", 0, 128), R("rp", 0, 128), R("e128", 0, 128)
-    for lane in (2, 3):
-        ms(R("rlt", lane, 512, 4), 0.0)
-        ms(R("rlt", 544 + lane, 1056, 4), 0.0)
     p0 = R("pi", 0, 1)
     ts(R("pi", 1, 2), p0, 15, None, A.bitwise_and)
     ts(R("pi", 2, 3), p0, 4, None, A.arith_shift_right)
     ts(R("pi", 3, 4), p0, 4, 1, A.arith_shift_right, A.bitwise_and)
-    cp(R("sc", 0, 4), R("pi", 0, 4))
-    ts(R("rlt", 0, 512, 4), TI, pF, None, A.is_ge)
-    act(R("rlt", 1, 512, 4), R("rlt", 0, 512, 4), F.Copy)
+    ts(R("pi", 4, 5), p0, 3, None, A.bitwise_and)
+    cp(R("sc", 0, 5), R("pi", 0, 5))
+    ms(R("pm", 0, 32), -9e29)
+    ms(R("xt", 512, 544), 0.0)
+    zero("rlt", 2, 1056, 544)
+    zero("rlt", 3, 1056, 544)
     ts(R("rlt", 544, 1056, 4), TI, pF, None, A.is_equal)
-    ts(R("rlt", 545, 1056, 4), TI, pF, 2.0, A.is_equal, A.mult)
+    act(R("rlt", 545, 1056, 4), R("rlt", 544, 1056, 4), F.Copy, 2.0)
+    ts(R("rlt", 0, 512, 4), TI, pF, None, A.is_ge)
+    zero("rlt", 2)
+    zero("rlt", 3)
+    act(R("rlt", 1, 512, 4), R("rlt", 0, 512, 4), F.Copy)
+    zero("tk", 2)
+    zero("tk", 3)
+    act(e100, eF, F.Identity, 1.0, 100.0)
+    act(iH, iF, F.Identity, 1.0, 0.5)
+    act(R("bib", 0, 3), R("bi", 0, 3), F.Identity, 1.0, iH)
     ts(R("rst", 0, 512, 4), RP, iF, None, A.is_equal)
     for lane in (1, 2, 3):
         act(R("rst", lane, 512, 4), R("rst", 0, 512, 4), F.Copy)
-    ms(R("xt", 512, 544), 0.0)
+    act(R("bt", 192, 512), R("rst", 192, 512), F.Copy, 0.0)
     ms(R("gt", 512, 544), 0.0)
-    ms(R("pm", 0, 1), -9e29)
-    ms(R("pm2", 0, 1), -9e29)
-    ms(R("z8", 0, 8), 0.0)
-    for lane in (2, 3):
-        ms(R("tk", lane, 512, 4), 0.0)
-    qz("rlq", 0, 128, "rlt", 0)
-    ts(R("bib", 0, 3), R("bi", 0, 3), iF, 0.5, A.add, A.add)
     ts(R("emv", 0, 16), R("em16", 0, 16), eF, None, A.is_equal)
-    ms(R("bt", 192, 512), 0.0)
-    ts(e100, eF, 100.0, None, A.add)
-    ts(R("bt", 2, 192, 4), R("g48", 0, 48), e100, 256.0, A.is_equal, A.mult)
-    ts(R("bt", 3, 192, 4), R("g48", 0, 48), e100, 16.0, A.is_equal, A.mult)
-    qz("rq", 0, 128, "rst")
-    qz("xq", 0, 136, "xt")
     qz("rlq", 128, 136, "rlt", 512)
+    qz("xq", 0, 136, "xt")
     mm("ps0", "xq", 0, "rlq", 128, 128)
+    qz("rlq", 0, 128, "rlt", 0)
 
     S = R("ps0", 0, 8)
     scan(R("pm", 1, 9), S, R("z8", 0, 8))
@@ -266,22 +278,25 @@ def rank_program(g, core, T, topo):
     ts(R("cm", 0, 9), R("pm", 0, 9), R("pm", 8, 9), BIG, A.is_equal, A.mult)
     tt(R("ab", 0, 8), R("cm", 1, 9), R("cm", 0, 8), A.subtract)
     tt(R("s2", 0, 8), S, R("ab", 0, 8), A.subtract)
-    scan(R("pm2", 1, 9), R("s2", 0, 8), R("z8", 0, 8))
-    act(R("junk", 8, 16), R("pm2", 1, 9), F.Sign, -1.0, R("pm2", 8, 9), R("iab", 1, 2))
+    scan(R("pm", 17, 25), R("s2", 0, 8), R("z8", 0, 8))
+    act(R("junk", 8, 16), R("pm", 17, 25), F.Sign, -1.0, R("pm", 24, 25), R("iab", 1, 2))
     ts(R("tk", 0, 512, 4), E128, R("iab", 0, 1), None, A.is_equal)
+    ts(R("bt", 2, 192, 4), R("g48", 0, 48), e100, 256.0, A.is_equal, A.mult)
+    act(R("bt", 3, 192, 4), R("bt", 2, 192, 4), F.Copy, 0.0625)
     ts(R("tk", 1, 512, 4), E128, R("iab", 1, 2), None, A.is_equal)
     qz("tkq", 0, 128, "tk")
 
     mm("ps1", "tkq", 0, "rlq", 0, 130)
     mm("ps2", "tkq", 0, "rlq", 0, 130)
     mm("ps3", "tkq", 0, "rlq", 134, 130)
+    qz("rq", 0, 128, "rst")
+    qz("xq", 136, 136, "gt")
     for k in range(2):
         act(R("junk", 16 + 128 * k, 144 + 128 * k), R("ps1", 0, 128), F.Sign, -1.0, R("bib", k, k + 1), R("acc", k, k + 1))
-    qz("xq", 136, 136, "gt")
     ts(R("tmpc", 0, 128), R("ps2", 0, 128), R("bib", 2, 3), 0.5, A.is_lt, A.subtract)
     red(R("acc", 2, 3), R("tmpc", 0, 128), A.add)
     for k in range(2):
-        ts(R("n48", k, 48, 3), R("emv", 0, 16), R("acc", k, k + 1), None, A.mult)
+        act(R("n48", k, 48, 3), R("emv", 0, 16), F.Copy, R("acc", k, k + 1))
     ts(R("n48", 2, 48, 3), R("emv", 0, 16), R("acc", 2, 3), 2.0, A.mult, A.mult)
     ts(R("bt", 0, 192, 4), R("n48", 0, 48), MAGIC16, MAGIC16, A.add, A.subtract)
     tt(R("bt", 1, 192, 4), R("n48", 0, 48), R("bt", 0, 192, 4), A.subtract)
@@ -290,84 +305,88 @@ def rank_program(g, core, T, topo):
     ts(R("off", 0, 48), R("ps4", 10, 58), 0.5, 64.0, A.mult, A.add)
 
     there = [T.rank_of(c) for c in far]
-    for group in (there, [e for e in range(N) if e not in there]):
+    for group in (there[:2], there[2:], [e for e in range(N) if e not in there]):
         for e in group:
             if e - 1 not in group:
                 n = 1
                 while e + n in group:
                     n += 1
                 pick("sl", 96 * e, 96 * n, "xq", 272, "off", 6 * e)
-    send("sl", 96, 0, 96, "ld", 96, "arc", True, far)
-    send("sl", 96, 0, 96, "ld", 96, "arc", True, near)
-    send("sl_s", 96, 0, 96, "ld_s", 96, "arp", False, peers)
+    out = lambda e: 96 * e
+    for to in (far[:2], far[2:], near):
+        send("sl", out, 96, "ld", "arc", True, to)
+    send("sl_s", out, 96, "ld_s", "arp", False, peers)
     localcopy("sl", 96 * q, "ld", 96 * q, 96, "owc", True)
     localcopy("sl_s", 96 * q, "ld_s", 96 * q, 96, "owp", False)
     arrives("ld", 96, "arc")
     arrives("ld_s", 96, "arp")
 
-    iota("s96", 96, [[16, 3], [0, 2], [1, 16]])
-    iota("h96", 96, [[0, 3], [1, 2], [0, 16]])
+    iota("blt", 576, [[0, 576]])
     iota("cp16", 16, [[20, 2], [1, 8]])
     iota("zer", 512, [[0, 512]])
-    iota("bt2", 640, [[0, 640]])
-    act(R("wt", 0, 128), R("ps3", 2, 130), F.Copy)
+    iota("bt2", 512, [[0, 512]])
     ts(R("eye", 4, 516, 4), TI, pF, None, A.is_equal)
     ms(R("ones", 0, 128), 1.0)
-    cp(R("sc", 16, 20), R("pb", 0, 4))
+    act(R("sc", 16, 20), R("pb", 0, 4), F.Copy)
     for b in range(4):
         act(R("prt", b, 512, 4), R("ones", 0, 128), F.Copy, col(16 + b))
     for b in range(4):
         qz("ebq", 128 * b, 128, "eye", 4 - b)
     qz("wq", 0, 512, "wb")
-    ts(R("ofx", 0, 24), R("fx", 0, 24), iF, None, A.add)
-    ts(R("ofg", 0, 24), R("fx", 0, 24), iF, 48.0, A.add, A.add)
+    ts(R("ofs", 0, 48), R("fx", 0, 48), iF, None, A.add)
     qz("prq", 0, 128, "prt")
+    act(R("wt", 0, 128), R("ps3", 2, 130), F.Copy)
+    ts(R("at", 3, 512, 4), RP, pF, None, A.is_equal)
+    ms(R("at", 512, 528), 0.0)
+    ts(flag, pF, float(q), 64.0, A.not_equal, A.mult)
+    act(R("at", 519, 528, 4), R("ones", 0, 3), F.Copy, flag)
+    act(R("s96", 0, 96), R("s96", 0, 96), F.Copy, -TINY)
+    act(R("sc", 9, 12), R("bib", 0, 3), F.Identity, TINY, -0.5 * TINY)
     ts(R("o96", 0, 96), R("h96", 0, 96), hF, -BIG, A.not_equal, A.mult)
-    ts(R("s96", 0, 96), R("s96", 0, 96), -TINY, None, A.mult)
-    ts(R("sc", 9, 12), R("bib", 0, 3), 0.5, TINY, A.subtract, A.mult)
+    qz("uq", 0, 512, "ubb")
     tt(R("o96", 0, 96), R("o96", 0, 96), R("s96", 0, 96), A.add)
     for k in range(3):
-        ts(R("cc", 96 * k, 96 * k + 96), R("o96", 0, 96), col(9 + k), None, A.add)
-    ms(R("at", 3, 512, 4), 1.0)
-    for lane in (1, 2):
-        ms(R("at", 512 + lane, 528, 4), 0.0)
-    ts(R("sc", 12, 13), pF, float(q), 64.0, A.not_equal, A.mult)
-    ts(R("at", 515, 528, 4), R("ones", 0, 4), R("sc", 12, 13), None, A.mult)
-    ms(R("rk", 3, 4), 0.0)
-    ms(R("blt", 0, 544), 0.0)
-    SI = R("si8", 0, 8)
+        act(R("cc", 96 * k, 96 * k + 96), R("o96", 0, 96), F.Identity, 1.0, col(9 + k))
+    act(e16, eF, F.Copy, 16.0)
+    D16 = R("d16", 0, 12)
+    ts(R("blt", 1, 48, 4), D16, e16, 128.0, A.is_equal, A.mult)
+    act(R("blt", 2, 48, 4), R("blt", 1, 48, 4), F.Copy, 2.0)
+    act(R("blt", 3, 48, 4), D16, F.Copy)
+    ts(R("blt", 64, 112, 4), D16, e16, iF, A.is_equal, A.mult)
     for k in (1, 2):
-        ts(R("blt", k, 32, 4), SI, eF, 128.0 * k, A.is_equal, A.mult)
-    ts(z16, pF, 0.0, 16.0, A.is_equal, A.mult)
-    ts(R("blt", 3, 32, 4), SI, z16, None, A.mult)
-    for k in range(3):
-        ts(R("blt", 32 + k, 64, 4), SI, eF, iF, A.is_equal, A.mult)
-    qz("blq", 0, 136, "blt")
-    ts(R("pi", 1, 2), p0, 3, None, A.bitwise_and)
-    ts(R("sc", 13, 14), R("pi", 1, 2), 512.0, None, A.add)
-    ts(R("of2", 0, 16, 2), R("ones", 0, 8), R("sc", 13, 14), None, A.mult)
-    qz("uq", 0, 512, "ubb")
-    qz("vq", 0, 128, "vb")
+        act(R("blt", 64 + k, 112, 4), R("blt", 64, 112, 4), F.Copy)
+    act(R("blt", 71, 112, 12), R("ones", 0, 4), F.Copy, fF)
+    ms(R("blt", 7, 48, 12), 512.0)
+    qz("blq", 0, 144, "blt")
+    zero("kt", 1)
+    zero("kt", 2)
+    act(R("tok", 0, 2), R("acc", 0, 2), F.Identity, 0.5, 64.0)
+    act(R("tok", 2, 3), R("acc", 2, 3), F.Identity, 1.0, 64.0)
+    k3 = lambda n: R(n, 0, 3)
+    act(k3("mp"), k3("tok"), F.Identity, 0.0625, -0.46875)
+    zero("oht", 3)
+    zero("aht", 3, 576, 64)
+    zero("aht", 3, 1088, 576)
+    act(R("aht", 0, 64), R("rst", 0, 64), F.Copy, 0.0)
 
     MK = lambda b, o: R("mk", 384 * b + o, 384 * b + o + 128)
-
-    def arrange(o):
-        pick("xe", o, 128, "ld", 768, "ofx", o // 16)
-        pick("ge", o, 128, "ld", 768, "ofg", o // 16)
-
-    arrange(0)
+    pick("xg", 0, 128, "ld", 768, "ofs", 0)
+    pick("xg", 128, 128, "ld", 768, "ofs", 8)
+    pick("xg", 256, 256, "ld", 768, "ofs", 16)
+    pickc("xg", 512, 256, "ld", 768, "ofs", 32)
     for o in (0, 128, 256):
         for i in range(4):
-            mm("ps%d" % i, "wq", 128 * i, "xe", o, 128)
-        if o < 256:
-            arrange(o + 128)
+            mm("ps%d" % i, "wq", 128 * i, "xg", 2 * o, 128)
         for b in range(4):
-            mm("ps%d" % (4 + b), "ebq", 128 * b, "ge", o, 128)
-        for b in (0, 2):
+            mm("ps%d" % (4 + b), "ebq", 128 * b, "xg", 2 * o + 128, 128)
+        left = (0, 2, 3) if o == 0 else (0, 2)
+        for b in left:
             ts(MK(b, o), R("ps%d" % b, 0, 128), 0.0, None, A.is_gt)
-        for j, b in enumerate((1, 3)):
+        for j, b in enumerate(b for b in range(4) if b not in left):
             act(R("sg", 384 * j + o, 384 * j + o + 128), R("ps%d" % b, 0, 128), F.Sign)
             act(MK(b, o), R("sg", 384 * j + o, 384 * j + o + 128), F.Relu)
+        if o == 0:
+            picks("xg", 512, 256, "ld", 768, "ofs", 32)
         for b in range(4):
             tt(R("mt", 4 * o + b, 4 * o + 512, 4), R("ps%d" % (4 + b), 0, 128), MK(b, o), A.mult)
         qz("mq", o, 128, "mt", 4 * o)
@@ -381,7 +400,7 @@ def rank_program(g, core, T, topo):
 
     def shrink(h, i):
         o, n = parts[h]
-        if i < 3:
+        if i < 3 + h:
             act(R("dxt", 4 * o + i, 4 * (o + n), 4), R(UB(h, i), 0, n), F.Copy, 0.0625)
         else:
             ts(R("dxt", 4 * o + i, 4 * (o + n), 4), R(UB(h, i), 0, n), 0.0625, None, A.mult)
@@ -407,91 +426,84 @@ def rank_program(g, core, T, topo):
     for k in (0, 1):
         act(R("junk", 96 * k, 96 * k + 96), C(k), F.Copy, acc=rk(k))
     red(rk(2), C(2), A.add)
-    for k in (0, 1, 2):
+    for k in (0, 2, 1):
         ts(R("at", k, 512, 4), RP, rk(k), None, A.is_equal)
-    cp(R("at", 512, 528, 4), R("rk", 0, 4))
+    cp(R("at", 516, 528, 4), R("rk", 0, 3))
     qz("dxw", 384, 132, "at")
     for i in (1, 2, 3):
         shrink(0, i)
     qz("dxw", 0, 256, "dxt")
     mm("ps4", "dxw", 384, "blq", 0, 128, True, False)
-    mm("ps4", "dxw", 384, "blq", 8, 128, False, True)
+    mm("ps4", "dxw", 384, "blq", 16, 128, False, True)
     for i in range(4):
         shrink(1, i)
+    cp(R("of2", 0, 12), R("ps4", 0, 12))
     qz("dxw", 256, 128, "dxt", 1024)
-    cp(R("of2", 1, 16, 2), R("ps4", 0, 8))
-    pick("ret", 0, 256, "dxw", 516, "of2", 0)
+    pick("ret", 0, 192, "dxw", 516, "of2", 0)
 
-    send("ret", 32, 12, 20, "rl", 20, "rec", True, peers)
-    send("ret_s", 32, 12, 20, "rl_s", 20, "rep", False, peers)
-    localcopy("ret", 32 * q + 12, "rl", 20 * q, 20, "orc", True)
-    localcopy("ret_s", 32 * q + 12, "rl_s", 20 * q, 20, "orp", False)
+    back = lambda d: 24 * d if d % 2 == 0 else 24 * d + 4
+    send("ret", back, 20, "rl", "rec", True, peers)
+    send("ret_s", back, 20, "rl_s", "rep", False, peers)
+    localcopy("ret", back(q), "rl", 20 * q, 20, "orc", True)
+    localcopy("ret_s", back(q), "rl_s", 20 * q, 20, "orp", False)
     arrives("rl", 20, "rec")
     arrives("rl_s", 20, "rep")
+    first, ranks = (0, 17) if q % 2 == 0 else (4, 1)
 
-    k3 = lambda n: R(n, 0, 3)
-    ts(R("tok", 0, 2), R("acc", 0, 2), 0.5, 64.0, A.mult, A.add)
-    ts(R("tok", 2, 3), R("acc", 2, 3), 64.0, None, A.add)
-    ms(R("oht", 3, 512, 4), 0.0)
-    ts(k3("mm_"), k3("tok"), 7.5, 0.0625, A.subtract, A.mult)
+    ts(k3("mm_"), k3("mp"), MAGIC1, MAGIC1, A.add, A.subtract)
+    act(k3("m16"), k3("mm_"), F.Copy, -16.0)
+    act(k3("m20"), k3("mm_"), F.Identity, 1.0, -20.0)
     for k in range(3):
         ts(R("oh", 128 * k, 128 * k + 128), TI, R("tok", k, k + 1), None, A.is_equal)
-    ts(k3("mm_"), k3("mm_"), MAGIC1, MAGIC1, A.add, A.subtract)
     for k in range(3):
         tt(R("oht", k, 512, 4), R("oh", 128 * k, 128 * k + 128), R("wt", 0, 128), A.mult)
         act(R("junk", 128 * k, 128 * k + 128), R("oht", k, 512, 4), F.Copy, acc=R("wk", k, k + 1))
-    ts(k3("rr_"), k3("mm_"), -16.0, None, A.mult)
-    ms(R("aht", 3, 1024, 4), 0.0)
-    tt(k3("rr_"), k3("rr_"), k3("tok"), A.add)
+    act(k3("w20"), k3("wk"), F.Copy, 20.0)
+    tt(k3("rr_"), k3("m16"), k3("tok"), A.add)
+    ts(eh, eF, 8.0, None, A.subtract)
     ts(qsel, eF, float(q), None, A.is_equal)
     for k in range(3):
-        ts(R("aht", 512 + k, 1024, 4), RP, R("rr_", k, k + 1), None, A.is_equal)
-        act(R("aht", k, 512, 4), R("aht", 512 + k, 1024, 4), F.Copy, 20.0)
+        ts(R("aht", 576 + k, 1088, 4), RP, R("rr_", k, k + 1), None, A.is_equal)
+        act(R("aht", 64 + k, 576, 4), R("aht", 576 + k, 1088, 4), F.Copy, 20.0)
     ts(R("kt", 0, 512, 4), RP, iF, qsel, A.is_equal, A.mult)
-    for lane in (1, 2):
-        ms(R("kt", lane, 512, 4), 0.0)
     ts(R("kt", 3, 512, 4), E128, pF, None, A.is_equal)
-    qz("kq", 0, 128, "kt")
-    ts(k3("cd"), k3("wk"), 20.0, -20.0, A.mult, A.add)
-    ts(eh, eF, 7.0, None, A.subtract)
-    tt(k3("cd"), k3("cd"), k3("mm_"), A.add)
-    qz("ahq", 0, 256, "aht")
-    for k in range(3):
-        ts(R("mka", 16 * k, 16 * k + 16), R("cp16", 0, 16), R("cd", k, k + 1), None, A.is_equal)
-        ts(R("mkh", 16 * k, 16 * k + 16), R("cp16", 0, 16), R("cd", k, k + 1), eh, A.is_equal, A.mult)
     qz("rl", 160, 128, "zer")
+    qz("kq", 0, 128, "kt")
+    tt(k3("cd"), k3("w20"), k3("m20"), A.add)
+    for k in range(3):
+        ts(R("aht", k, 64, 4), R("cp16", 0, 16), R("cd", k, k + 1), eh, A.is_equal, A.mult)
+        ts(R("mka", 16 * k, 16 * k + 16), R("cp16", 0, 16), R("cd", k, k + 1), None, A.is_equal)
+    qz("ahq", 0, 272, "aht")
     qz("ohq", 0, 128, "oht")
+    qz("vq", 0, 128, "vb")
+    mm("ps1", "ahq", 16, "ahq", 0, 128, True, False)
 
     mm("ps0", "kq", 0, "rl", 0, 160)
     for k in range(3):
-        red(R("rkh", k, k + 1), R("ps0", k, 160, 20), A.min)
-    ts(k3("rth"), k3("rkh"), 15.5, None, A.is_lt)
-    ts(k3("rrh"), k3("rkh"), 16.0, 16.0, A.min, A.subtract)
+        red(R("rkh", k, k + 1), R("ps0", ranks + k, 160, 20), A.min)
     for k in range(3):
-        act(R("bt2", k, 64, 4), R("mkh", 16 * k, 16 * k + 16), F.Copy, R("rth", k, k + 1))
-    cp(R("bt2", 128, 131), k3("rth"))
-    for k in range(3):
-        ts(R("bt2", 64 + k, 128, 4), R("mka", 16 * k, 16 * k + 16), R("rrh", k, k + 1), None, A.mult)
-    qz("btq", 0, 160, "bt2")
-    mm("ps1", "ahq", 0, "btq", 0, 128, True, False)
-    mm("ps1", "ahq", 128, "btq", 16, 128, False, True)
-    mm("ps2", "btq", 32, "ohq", 0, 128)
-    ts(R("of3", 0, 16), R("ps1", 0, 16), 160.0, None, A.add)
+        ts(R("bt2", k, 64, 4), R("mka", 16 * k, 16 * k + 16), R("rkh", k, k + 1), 16.0, A.mult, A.min)
+    qz("btq", 0, 128, "bt2")
+    mm("ps1", "ahq", 144, "btq", 0, 128, False, True)
+    ts(R("of3", 0, 16), R("ps1", 0, 16), 160.0 + first, None, A.add)
     for h in range(2):
-        pick("zc", 128 * h, 128, "rl", 162, "of3", 8 * h)
+        pick("zc", 128 * h, 128, "rl", 168, "of3", 8 * h)
         for b in range(4):
             mm("ps%d" % (4 + b), "ebq", 128 * b, "zc", 128 * h, 128, h == 0, h == 1)
-    act(R("ctsb", 0, 128), R("ps2", 0, 128), F.Copy)
-    dma("y", [R("ctsb", 0, 128)], [], T.ct[:, :], T.ctsb[0:1, 0:128], "o_ct")
+    ts(R("bt2", 64, 67), k3("rkh"), 15.5, None, A.is_lt)
+    qz("ctq", 0, 128, "bt2")
+    mm("ps2", "ctq", 0, "ohq", 0, 128)
     for b in (0, 2):
         act(R("zt", b, 512, 4), R("ps%d" % (4 + b), 0, 128), F.Copy)
     for b in (1, 3):
         cp(R("zt", b, 512, 4), R("ps%d" % (4 + b), 0, 128))
     qz("zq", 0, 128, "zt")
     mm("ps3", "vq", 0, "zq", 0, 128)
+    act(R("ctsb", 0, 128), R("ps2", 0, 128), F.Copy)
     dma("y", [R("zq", 0, 128)], [], T.oc[:, :], T.zq[:, 0:128].bitcast(dt.uint8), "o_oc")
     for k in range(4):
         dma("y" if k < 1 else "s", [R("zq_s", 0, 128)], [], T.osc[4 * k:4 * k + 4, 0:128], T.zq_s[32 * k:32 * k + 4, 0:128], "o_s%d" % k)
+    dma("s", [R("ctsb", 0, 128)], [], T.ct[:, :], T.ctsb[16:17, 0:128], "o_ct")
     cp(R("ysb", 0, 128), R("ps3", 0, 128))
     dma("y", [R("ysb", 0, 128)], [], T.y[:, :], T.ysb[:, 0:128], "o_y")
 

@@ -3,7 +3,7 @@ from concourse.mybir import dt, AluOpType, AxisListType, ActivationFunctionType
 
 A = AluOpType
 F = ActivationFunctionType
-BIG, TINY, MAGIC16, MAGIC1 = 1e29, 2.0 ** -100, 1.5 * 2.0 ** 27, 1.5 * 2.0 ** 23
+BIG, FLOOR, TINY, MAGIC16, MAGIC1 = 1e29, -1e25, 2.0 ** -100, 1.5 * 2.0 ** 27, 1.5 * 2.0 ** 23
 
 SCRATCH = {}
 ALIAS = {}
@@ -18,32 +18,34 @@ def _mx(name, n):
     _sb(name + "_s", n, "uint8")
 
 
-for _n, _w in (("xq", 400), ("rlq", 264), ("tkq", 128), ("rq", 128), ("sl", 768), ("ld", 768), ("xg", 768), ("wq", 512),
-               ("uq", 512), ("vq", 128), ("prq", 128), ("ebq", 512), ("mq", 384), ("dxw", 516), ("blq", 144), ("ret", 192), ("rl", 288),
-               ("kq", 128), ("ahq", 272), ("ohq", 128), ("btq", 128), ("ctq", 128), ("zc", 256), ("zq", 128)):
+for _n, _w in (("xq", 664), ("tkq", 128), ("rq", 128), ("sl", 768), ("ld", 768), ("xg", 768), ("wq", 512),
+               ("uq", 512), ("prq", 128), ("ebq", 512), ("mq", 384), ("dxw", 516), ("blq", 144), ("ret", 192), ("rl", 152), ("rv", 160),
+               ("kq", 128), ("ahq", 160), ("ohq", 128), ("btq", 128), ("ctq", 128), ("zc", 256), ("zq", 128)):
     _mx(_n, _w)
-for _n, _w in (("xt", 544), ("gt", 544), ("rlt", 1056), ("tk", 512), ("bt", 512), ("rst", 512), ("wb", 2048), ("ubb", 2048), ("vb", 512),
-               ("pb", 4), ("prt", 512), ("eye", 520), ("mt", 1536), ("dxt", 1536), ("blt", 576), ("at", 528), ("kt", 512), ("aht", 1088),
-               ("oht", 512), ("bt2", 512), ("zt", 512), ("zer", 512), ("ones", 128), ("ti", 128), ("e128", 128), ("rp", 128), ("tmpc", 128),
-               ("wt", 128), ("oh", 384), ("mk", 1536), ("sg", 768), ("junk", 384), ("mka", 48), ("dd", 288), ("cmp", 288), ("cc", 288)):
+for _n, _w in (("xt", 576), ("gt", 544), ("tri", 512), ("tk", 512), ("br", 704), ("wb", 2048), ("ubb", 2048), ("bv", 640),
+               ("pb", 4), ("bp", 640), ("eye", 520), ("mt", 1536), ("dxt", 1536), ("at", 528), ("aht", 640),
+               ("oht", 512), ("zt", 512), ("ti", 128), ("e128", 128), ("rp", 128), ("tmpc", 128), ("oa", 384),
+               ("oh", 384), ("mk", 1536), ("sg", 768), ("junk", 384), ("dd", 288), ("cmp", 288), ("cc", 288)):
     _sb(_n, _w, "bfloat16")
-for _n, _w in (("sc", 32), ("pm", 32), ("cm", 16), ("ab", 8), ("s2", 8), ("iab", 4), ("acc", 4), ("n48", 48), ("ys", 96), ("t96", 96),
-               ("rk", 4), ("tok", 4), ("mp", 4), ("mm_", 4), ("m16", 4), ("m20", 4), ("rr_", 4), ("wk", 4), ("w20", 4), ("cd", 4), ("rkh", 4),
-               ("ysb", 128), ("ctsb", 128)):
+for _n, _w in (("sc", 32), ("pm", 40), ("cm", 16), ("ab", 8), ("iab", 4), ("acc", 4), ("n48", 48), ("ys", 96), ("t96", 96),
+               ("rk", 4), ("tok", 4), ("nt", 4), ("mp", 4), ("mm_", 4), ("m16", 4), ("m18", 4), ("rr_", 4), ("wk", 4), ("w18", 4),
+               ("cd", 4), ("rkh", 4), ("ysb", 128), ("ctsb", 128)):
     _sb(_n, _w)
 _at = 0
 for _n, _w in (("em16", 16), ("emv", 16), ("g48", 48), ("bi", 16), ("bib", 16), ("d16", 16), ("cp16", 16), ("s96", 96), ("h96", 96),
-               ("o96", 96), ("fx", 48), ("z8", 16)):
+               ("o96", 96), ("fx", 48)):
     ALIAS[_n] = ("cs", _at)
     _at += _w
 _sb("cs", _at)
+for _n, _b, _o in (("bt", "br", 0), ("rst", "br", 192), ("blt", "bp", 0), ("prt", "bp", 128), ("bt2", "bv", 0)):
+    ALIAS[_n] = (_b, _o)
 _sb("pi", 8, "int32")
 for _n, _w in (("off", 48), ("ofs", 48), ("of2", 16), ("of3", 16)):
     _sb(_n, _w, "uint16")
 for _k in range(8):
     SCRATCH["ps%d" % _k] = ("psum", [128, 512], "float32")
 SEMAPHORES = ["sv", "ss", "st", "sg", "lx", "lrt", "lgr", "lpr", "lw", "lub", "lv", "arc", "arp", "owc", "owp", "rec", "rep", "orc", "orp",
-              "loc", "o_oc", "o_y", "o_ct", "o_s0", "o_s1", "o_s2", "o_s3"]
+              "rkc", "rkp", "okc", "okp", "zrc", "zrp", "loc", "o_oc", "o_y", "o_ct", "o_s0", "o_s1", "o_s2", "o_s3"]
 
 
 def rank_program(g, core, T, topo):
@@ -137,12 +139,13 @@ def rank_program(g, core, T, topo):
     def red(out, a, o):
         op("v", [a], [out], lambda: g.vector.tensor_reduce(ap(out), ap(a), AxisListType.X, o))
 
-    def scan(out, a, z):
-        op("v", [a, z], [out], lambda: g.vector.tensor_tensor_scan(ap(out), ap(a), ap(z), -9e29, A.max, A.add))
+    def scan(out, a, z, o0, o1):
+        op("v", [a, z], [out], lambda: g.vector.tensor_tensor_scan(ap(out), ap(a), ap(z), -9e29, o0, o1))
 
     def qz(name, lo, n, tile, t0=0):
-        op("v", [R(tile, t0, t0 + 4 * n)], [R(name, lo, lo + n), R(name + "_s", lo, lo + n)],
-           lambda: g.vector.quantize_mx(T[name][:, lo:lo + n], T[name + "_s"][:, lo:lo + n], T[tile][:, t0:t0 + 4 * n]))
+        r = R(tile, t0, t0 + 4 * n)
+        op("v", [r], [R(name, lo, lo + n), R(name + "_s", lo, lo + n)],
+           lambda: g.vector.quantize_mx(T[name][:, lo:lo + n], T[name + "_s"][:, lo:lo + n], ap(r)))
 
     def act(out, a, f, scale=1.0, bias=0.0, acc=None):
         if acc is None:
@@ -159,15 +162,15 @@ def rank_program(g, core, T, topo):
            lambda: g.tensor.matmul_mx(T[bank][:, 0:n], T[lhs][:, l0:l0 + 128], T[lhs + "_s"][:, l0:l0 + 128],
                                       T[rhs][:, r0:r0 + n], T[rhs + "_s"][:, r0:r0 + n], start, stop))
 
-    def pickc(out, o0, n, win, w1, off, f0):
+    def pickc(out, o0, n, win, w0, w1, off, f0):
         fr = R(off, f0, f0 + n // 16)
-        op("v", [R(win, 0, w1), fr], [R(out, o0, o0 + n)],
-           lambda: g.vector.tensor_copy(T[out][:, o0:o0 + n].bitcast(dt.uint32), T[win][:, 0:w1].bitcast(dt.uint32).indirect(ap(fr))))
+        op("v", [R(win, w0, w1), fr], [R(out, o0, o0 + n)],
+           lambda: g.vector.tensor_copy(T[out][:, o0:o0 + n].bitcast(dt.uint32), T[win][:, w0:w1].bitcast(dt.uint32).indirect(ap(fr))))
 
-    def picks(out, o0, n, win, w1, off, f0):
+    def picks(out, o0, n, win, w0, w1, off, f0):
         fr = R(off, f0, f0 + n // 16)
-        op("s", [R(win + "_s", 0, w1), fr], [R(out + "_s", o0, o0 + n)],
-           lambda: g.scalar.activation(T[out + "_s"][:, o0:o0 + n], T[win + "_s"][:, 0:w1].indirect(ap(fr)), F.Copy))
+        op("s", [R(win + "_s", w0, w1), fr], [R(out + "_s", o0, o0 + n)],
+           lambda: g.scalar.activation(T[out + "_s"][:, o0:o0 + n], T[win + "_s"][:, w0:w1].indirect(ap(fr)), F.Copy))
 
     def pick(*a):
         pickc(*a)
@@ -213,96 +216,108 @@ def rank_program(g, core, T, topo):
         dma("y", [R(src, a, a + width)], [R(dst, b, b + width)], o, i, s)
 
     def load(qn, name, w, src, s, at=0):
-        dma(qn, [], [R(name, at, at + w)], T[name][:, at:at + w], src, s)
+        r = R(name, at, at + w)
+        dma(qn, [], [r], ap(r), src, s)
 
     load("y", "xt", 512, T.x[:, :], "lx")
-    load("s", "rlt", 32, T.rt[:, 0:32], "lrt", 512)
+    load("s", "xt", 32, T.rt[:, 0:32], "lrt", 544)
     load("y", "gt", 512, T.gr[:, :], "lgr")
     load("s", "pb", 4, T.pr[:, 0:4], "lpr")
     load("y", "wb", 2048, T.w[:, :], "lw")
     load("s", "ubb", 2048, T.ub[:, :], "lub")
-    load("y", "vb", 512, T.v[:, :], "lv")
+    load("y", "bv", 512, T.v[:, :], "lv", 128)
 
     iota("pi", 1, [[1, 1]], cm=1)
     iota("ti", 128, [[1, 128]])
     iota("rp", 128, [[0, 8], [1, 16]])
+    iota("bi", 3, [[16, 3]])
     iota("em16", 16, [[1, 8], [0, 2]])
     iota("g48", 48, [[1, 8], [100, 2], [0, 3]])
-    iota("bi", 3, [[16, 3]])
-    iota("z8", 8, [[0, 8]])
     iota("e128", 128, [[1, 8], [0, 16]])
-    iota("eye", 520, [[0, 520]])
     iota("fx", 48, [[16, 3], [48, 2], [96, 8]])
     iota("d16", 12, [[32, 4], [8, 3]])
     iota("s96", 96, [[16, 3], [0, 2], [1, 16]])
     iota("h96", 96, [[0, 3], [1, 2], [0, 16]])
+    iota("cp16", 16, [[18, 2], [1, 8]])
+    iota("blt", 128, [[0, 128]])
     col = lambda k: R("sc", k, k + 1)
-    pF, iF, eF, hF, fF, e100, iH, flag, e16 = [col(k) for k in range(9)]
-    eh, qsel = col(12), col(13)
+    pF, iF, eF, hF, e100, iH, flag, e16, eh, el, qsel = [col(k) for k in (0, 1, 2, 3, 5, 6, 7, 8, 12, 13, 14)]
     TI, RP, E128 = R("ti", 0, 128), R("rp", 0, 128), R("e128", 0, 128)
     p0 = R("pi", 0, 1)
+    ms(R("xt", 512, 544), 0.0)
+    ms(R("pm", 0, 40), FLOOR)
+    ms(R("gt", 512, 544), 0.0)
     ts(R("pi", 1, 2), p0, 15, None, A.bitwise_and)
     ts(R("pi", 2, 3), p0, 4, None, A.arith_shift_right)
     ts(R("pi", 3, 4), p0, 4, 1, A.arith_shift_right, A.bitwise_and)
-    ts(R("pi", 4, 5), p0, 3, None, A.bitwise_and)
-    cp(R("sc", 0, 5), R("pi", 0, 5))
-    ms(R("pm", 0, 32), -9e29)
-    ms(R("xt", 512, 544), 0.0)
-    zero("rlt", 2, 1056, 544)
-    zero("rlt", 3, 1056, 544)
-    ts(R("rlt", 544, 1056, 4), TI, pF, None, A.is_equal)
-    act(R("rlt", 545, 1056, 4), R("rlt", 544, 1056, 4), F.Copy, 2.0)
-    ts(R("rlt", 0, 512, 4), TI, pF, None, A.is_ge)
-    zero("rlt", 2)
-    zero("rlt", 3)
-    act(R("rlt", 1, 512, 4), R("rlt", 0, 512, 4), F.Copy)
+    ms(R("eye", 0, 520), 0.0)
+    cp(R("sc", 0, 4), R("pi", 0, 4))
+    ts(R("eye", 4, 516, 4), TI, pF, None, A.is_equal)
+    for lane in range(4):
+        ts(R("tri", lane, 512, 4), TI, pF, None, A.is_ge)
+    for lane in range(4):
+        ts(R("rst", lane, 512, 4), RP, iF, None, A.is_equal)
     zero("tk", 2)
     zero("tk", 3)
+    zero("oht", 3)
+    zero("aht", 3, 640, 128)
+    act(R("aht", 0, 128), TI, F.Copy, 0.0)
     act(e100, eF, F.Identity, 1.0, 100.0)
     act(iH, iF, F.Identity, 1.0, 0.5)
+    act(e16, eF, F.Copy, 16.0)
     act(R("bib", 0, 3), R("bi", 0, 3), F.Identity, 1.0, iH)
-    ts(R("rst", 0, 512, 4), RP, iF, None, A.is_equal)
-    for lane in (1, 2, 3):
-        act(R("rst", lane, 512, 4), R("rst", 0, 512, 4), F.Copy)
-    act(R("bt", 192, 512), R("rst", 192, 512), F.Copy, 0.0)
-    ms(R("gt", 512, 544), 0.0)
-    ts(R("emv", 0, 16), R("em16", 0, 16), eF, None, A.is_equal)
-    qz("rlq", 128, 136, "rlt", 512)
-    qz("xq", 0, 136, "xt")
-    mm("ps0", "xq", 0, "rlq", 128, 128)
-    qz("rlq", 0, 128, "rlt", 0)
+    qz("xq", 128, 144, "xt")
+    mm("ps0", "xq", 128, "xq", 144, 128)
+    qz("xq", 272, 128, "tri")
+    qz("ebq", 0, 128, "eye", 4)
+    ts(R("bt", 2, 192, 4), R("g48", 0, 48), e100, 512.0, A.is_equal, A.mult)
+    act(R("bt", 3, 192, 4), R("bt", 2, 192, 4), F.Copy, 0.0625)
 
-    S = R("ps0", 0, 8)
-    scan(R("pm", 1, 9), S, R("z8", 0, 8))
+    S = R("ps0", 120, 128)
+    ts(R("emv", 0, 16), R("em16", 0, 16), eF, None, A.is_equal)
+    scan(R("pm", 1, 9), S, R("pm", 32, 40), A.max, A.max)
     act(R("junk", 0, 8), R("pm", 1, 9), F.Sign, -1.0, R("pm", 8, 9), R("iab", 0, 1))
-    ts(R("cm", 0, 9), R("pm", 0, 9), R("pm", 8, 9), BIG, A.is_equal, A.mult)
-    tt(R("ab", 0, 8), R("cm", 1, 9), R("cm", 0, 8), A.subtract)
-    tt(R("s2", 0, 8), S, R("ab", 0, 8), A.subtract)
-    scan(R("pm", 17, 25), R("s2", 0, 8), R("z8", 0, 8))
+    ts(R("cm", 0, 8), R("pm", 1, 9), R("pm", 8, 9), BIG, A.is_lt, A.mult)
+    tt(R("ab", 0, 8), R("cm", 0, 8), R("pm", 0, 8), A.add)
+    scan(R("pm", 17, 25), S, R("ab", 0, 8), A.max, A.min)
     act(R("junk", 8, 16), R("pm", 17, 25), F.Sign, -1.0, R("pm", 24, 25), R("iab", 1, 2))
     ts(R("tk", 0, 512, 4), E128, R("iab", 0, 1), None, A.is_equal)
-    ts(R("bt", 2, 192, 4), R("g48", 0, 48), e100, 256.0, A.is_equal, A.mult)
-    act(R("bt", 3, 192, 4), R("bt", 2, 192, 4), F.Copy, 0.0625)
     ts(R("tk", 1, 512, 4), E128, R("iab", 1, 2), None, A.is_equal)
     qz("tkq", 0, 128, "tk")
 
-    mm("ps1", "tkq", 0, "rlq", 0, 130)
-    mm("ps2", "tkq", 0, "rlq", 0, 130)
-    mm("ps3", "tkq", 0, "rlq", 134, 130)
+    k3 = lambda n: R(n, 0, 3)
+    mm("ps1", "tkq", 0, "xq", 270, 130)
+    mm("ps2", "tkq", 0, "xq", 270, 130)
     qz("rq", 0, 128, "rst")
-    qz("xq", 136, 136, "gt")
+    qz("xq", 400, 136, "gt")
+    qz("ebq", 128, 128, "eye", 3)
     for k in range(2):
-        act(R("junk", 16 + 128 * k, 144 + 128 * k), R("ps1", 0, 128), F.Sign, -1.0, R("bib", k, k + 1), R("acc", k, k + 1))
-    ts(R("tmpc", 0, 128), R("ps2", 0, 128), R("bib", 2, 3), 0.5, A.is_lt, A.subtract)
+        act(R("junk", 16 + 128 * k, 144 + 128 * k), R("ps1", 2, 130), F.Sign, -1.0, R("bib", k, k + 1), R("acc", k, k + 1))
+    ts(R("tmpc", 0, 128), R("ps2", 2, 130), R("bib", 2, 3), 0.5, A.is_lt, A.subtract)
+    ts(R("ofs", 0, 48), R("fx", 0, 48), iF, None, A.add)
     red(R("acc", 2, 3), R("tmpc", 0, 128), A.add)
     for k in range(2):
         act(R("n48", k, 48, 3), R("emv", 0, 16), F.Copy, R("acc", k, k + 1))
+    ts(R("prt", 0, 512, 4), TI, 0.0, R("pb", 0, 1), A.mult, A.add)
     ts(R("n48", 2, 48, 3), R("emv", 0, 16), R("acc", 2, 3), 2.0, A.mult, A.mult)
+    ts(R("prt", 1, 512, 4), TI, 0.0, R("pb", 1, 2), A.mult, A.add)
     ts(R("bt", 0, 192, 4), R("n48", 0, 48), MAGIC16, MAGIC16, A.add, A.subtract)
+    ts(R("prt", 2, 512, 4), TI, 0.0, R("pb", 2, 3), A.mult, A.add)
     tt(R("bt", 1, 192, 4), R("n48", 0, 48), R("bt", 0, 192, 4), A.subtract)
-    qz("xq", 272, 128, "bt")
-    mm("ps4", "rq", 0, "xq", 262, 128)
+    ts(R("prt", 3, 512, 4), TI, 0.0, R("pb", 3, 4), A.mult, A.add)
+    qz("xq", 536, 128, "bt")
+    mm("ps4", "rq", 0, "xq", 526, 128)
+    for b in (2, 3):
+        qz("ebq", 128 * b, 128, "eye", 4 - b)
     ts(R("off", 0, 48), R("ps4", 10, 58), 0.5, 64.0, A.mult, A.add)
+    act(R("s96", 0, 96), R("s96", 0, 96), F.Copy, -TINY)
+    act(R("sc", 9, 12), R("bib", 0, 3), F.Identity, TINY, -0.5 * TINY)
+    act(R("tok", 0, 2), R("acc", 0, 2), F.Identity, 0.5, 64.0)
+    act(R("tok", 2, 3), R("acc", 2, 3), F.Identity, 1.0, 64.0)
+    act(k3("nt"), k3("tok"), F.Copy, -1.0)
+    act(k3("mp"), k3("tok"), F.Identity, 0.0625, -0.46875)
+    for k in range(3):
+        act(R("oa", 128 * k, 128 * k + 128), TI, F.Abs, 1.0, R("nt", k, k + 1))
 
     there = [T.rank_of(c) for c in far]
     for group in (there[:2], there[2:], [e for e in range(N) if e not in there]):
@@ -311,183 +326,189 @@ def rank_program(g, core, T, topo):
                 n = 1
                 while e + n in group:
                     n += 1
-                pick("sl", 96 * e, 96 * n, "xq", 272, "off", 6 * e)
+                pick("sl", 96 * e, 96 * n, "xq", 128, 536, "off", 6 * e)
     out = lambda e: 96 * e
     for to in (far[:2], far[2:], near):
         send("sl", out, 96, "ld", "arc", True, to)
     send("sl_s", out, 96, "ld_s", "arp", False, peers)
     localcopy("sl", 96 * q, "ld", 96 * q, 96, "owc", True)
     localcopy("sl_s", 96 * q, "ld_s", 96 * q, 96, "owp", False)
+    localcopy("xq", 256, "rl", 144, 8, "zrc", True)
+    localcopy("xq_s", 256, "rl_s", 144, 8, "zrp", False)
     arrives("ld", 96, "arc")
     arrives("ld_s", 96, "arp")
 
-    iota("blt", 576, [[0, 576]])
-    iota("cp16", 16, [[20, 2], [1, 8]])
-    iota("zer", 512, [[0, 512]])
-    iota("bt2", 512, [[0, 512]])
-    ts(R("eye", 4, 516, 4), TI, pF, None, A.is_equal)
-    ms(R("ones", 0, 128), 1.0)
-    act(R("sc", 16, 20), R("pb", 0, 4), F.Copy)
-    for b in range(4):
-        act(R("prt", b, 512, 4), R("ones", 0, 128), F.Copy, col(16 + b))
-    for b in range(4):
-        qz("ebq", 128 * b, 128, "eye", 4 - b)
-    qz("wq", 0, 512, "wb")
-    ts(R("ofs", 0, 48), R("fx", 0, 48), iF, None, A.add)
+    iota("bt2", 128, [[0, 128]])
     qz("prq", 0, 128, "prt")
-    act(R("wt", 0, 128), R("ps3", 2, 130), F.Copy)
+    ts(R("tri", 0, 512, 4), TI, pF, None, A.is_equal)
+    ts(R("tri", 1, 512, 4), TI, pF, 2.0, A.is_equal, A.mult)
+    ts(R("o96", 0, 96), R("h96", 0, 96), hF, -BIG, A.not_equal, A.mult)
     ts(R("at", 3, 512, 4), RP, pF, None, A.is_equal)
+    qz("xq", 0, 128, "tri")
     ms(R("at", 512, 528), 0.0)
     ts(flag, pF, float(q), 64.0, A.not_equal, A.mult)
-    act(R("at", 519, 528, 4), R("ones", 0, 3), F.Copy, flag)
-    act(R("s96", 0, 96), R("s96", 0, 96), F.Copy, -TINY)
-    act(R("sc", 9, 12), R("bib", 0, 3), F.Identity, TINY, -0.5 * TINY)
-    ts(R("o96", 0, 96), R("h96", 0, 96), hF, -BIG, A.not_equal, A.mult)
-    qz("uq", 0, 512, "ubb")
     tt(R("o96", 0, 96), R("o96", 0, 96), R("s96", 0, 96), A.add)
-    for k in range(3):
-        act(R("cc", 96 * k, 96 * k + 96), R("o96", 0, 96), F.Identity, 1.0, col(9 + k))
-    act(e16, eF, F.Copy, 16.0)
     D16 = R("d16", 0, 12)
     ts(R("blt", 1, 48, 4), D16, e16, 128.0, A.is_equal, A.mult)
+    ts(R("blt", 64, 112, 4), D16, e16, iF, A.is_equal, A.mult)
+    mm("ps3", "tkq", 0, "xq", 0, 130)
+    for k in range(3):
+        act(R("oh", 128 * k, 128 * k + 128), R("oa", 128 * k, 128 * k + 128), F.Relu, -1.0, 1.0)
     act(R("blt", 2, 48, 4), R("blt", 1, 48, 4), F.Copy, 2.0)
     act(R("blt", 3, 48, 4), D16, F.Copy)
-    ts(R("blt", 64, 112, 4), D16, e16, iF, A.is_equal, A.mult)
     for k in (1, 2):
         act(R("blt", 64 + k, 112, 4), R("blt", 64, 112, 4), F.Copy)
-    act(R("blt", 71, 112, 12), R("ones", 0, 4), F.Copy, fF)
+    act(R("at", 517, 528, 4), R("ti", 0, 3), F.Identity, 0.0, flag)
+    for k in range(3):
+        act(R("cc", 96 * k, 96 * k + 96), R("o96", 0, 96), F.Identity, 1.0, col(9 + k))
+    qz("wq", 0, 512, "wb")
     ms(R("blt", 7, 48, 12), 512.0)
+    ts(k3("mm_"), k3("mp"), MAGIC1, MAGIC1, A.add, A.subtract)
+    for k in range(3):
+        tt(R("oht", k, 512, 4), R("ps3", 0, 128), R("oh", 128 * k, 128 * k + 128), A.mult)
+    qz("uq", 0, 512, "ubb")
     qz("blq", 0, 144, "blt")
-    zero("kt", 1)
-    zero("kt", 2)
-    act(R("tok", 0, 2), R("acc", 0, 2), F.Identity, 0.5, 64.0)
-    act(R("tok", 2, 3), R("acc", 2, 3), F.Identity, 1.0, 64.0)
-    k3 = lambda n: R(n, 0, 3)
-    act(k3("mp"), k3("tok"), F.Identity, 0.0625, -0.46875)
-    zero("oht", 3)
-    zero("aht", 3, 576, 64)
-    zero("aht", 3, 1088, 576)
-    act(R("aht", 0, 64), R("rst", 0, 64), F.Copy, 0.0)
+    act(k3("m16"), k3("mm_"), F.Copy, -16.0)
+    act(k3("m18"), k3("mm_"), F.Identity, 1.0, -18.0)
+    ts(qsel, eF, float(q), None, A.is_equal)
+    ts(eh, eF, 8.0, 16.0, A.subtract, A.mult)
+    ts(el, eF, 8.0, 2.0, A.subtract, A.mult)
+    ts(R("tk", 1, 512, 4), E128, pF, None, A.is_equal)
+    ts(R("tk", 0, 512, 4), RP, iF, qsel, A.is_equal, A.mult)
+    tt(k3("rr_"), k3("m16"), k3("tok"), A.add)
+    qz("rv", 32, 128, "bv", 128)
+    qz("kq", 0, 128, "tk")
 
     MK = lambda b, o: R("mk", 384 * b + o, 384 * b + o + 128)
-    pick("xg", 0, 128, "ld", 768, "ofs", 0)
-    pick("xg", 128, 128, "ld", 768, "ofs", 8)
-    pick("xg", 256, 256, "ld", 768, "ofs", 16)
-    pickc("xg", 512, 256, "ld", 768, "ofs", 32)
+    pick("xg", 0, 128, "ld", 0, 768, "ofs", 0)
+    pick("xg", 128, 128, "ld", 0, 768, "ofs", 8)
+    pick("xg", 256, 256, "ld", 0, 768, "ofs", 16)
+    pickc("xg", 512, 256, "ld", 0, 768, "ofs", 32)
     for o in (0, 128, 256):
         for i in range(4):
             mm("ps%d" % i, "wq", 128 * i, "xg", 2 * o, 128)
         for b in range(4):
             mm("ps%d" % (4 + b), "ebq", 128 * b, "xg", 2 * o + 128, 128)
-        left = (0, 2, 3) if o == 0 else (0, 2)
-        for b in left:
+        for b in (0, 2):
             ts(MK(b, o), R("ps%d" % b, 0, 128), 0.0, None, A.is_gt)
-        for j, b in enumerate(b for b in range(4) if b not in left):
+        for j, b in enumerate((1, 3)):
             act(R("sg", 384 * j + o, 384 * j + o + 128), R("ps%d" % b, 0, 128), F.Sign)
             act(MK(b, o), R("sg", 384 * j + o, 384 * j + o + 128), F.Relu)
         if o == 0:
-            picks("xg", 512, 256, "ld", 768, "ofs", 32)
+            picks("xg", 512, 256, "ld", 0, 768, "ofs", 32)
         for b in range(4):
             tt(R("mt", 4 * o + b, 4 * o + 512, 4), R("ps%d" % (4 + b), 0, 128), MK(b, o), A.mult)
         qz("mq", o, 128, "mt", 4 * o)
 
     parts = ((0, 256), (256, 128))
-    UB = lambda h, i: "ps%d" % (4 - 4 * h + i)
+    UB = (("ps2", "ps3", "ps5", "ps6"), ("ps7", "ps0", "ps1", "ps4"))
 
-    def products(h):
-        for i in range(4):
-            mm(UB(h, i), "uq", 128 * i, "mq", parts[h][0], parts[h][1])
+    def product(h, i):
+        mm(UB[h][i], "uq", 128 * i, "mq", parts[h][0], parts[h][1])
 
-    def shrink(h, i):
+    def shrink(qn, h, i):
         o, n = parts[h]
-        if i < 3 + h:
-            act(R("dxt", 4 * o + i, 4 * (o + n), 4), R(UB(h, i), 0, n), F.Copy, 0.0625)
+        if qn == "s":
+            act(R("dxt", 4 * o + i, 4 * (o + n), 4), R(UB[h][i], 0, n), F.Copy, 0.0625)
         else:
-            ts(R("dxt", 4 * o + i, 4 * (o + n), 4), R(UB(h, i), 0, n), 0.0625, None, A.mult)
+            ts(R("dxt", 4 * o + i, 4 * (o + n), 4), R(UB[h][i], 0, n), 0.0625, None, A.mult)
 
-    for k in range(3):
-        mm("ps%d" % k, "mq", 128 * k, "prq", 0, 128)
-    products(0)
-    for k in range(3):
-        act(R("ys", 32 * k, 32 * k + 32), R("ps%d" % k, 0, 32), F.Abs)
-    products(1)
-    op("v", [R("ys", 0, 96)], [R("t96", 0, 96)], lambda: g.vector.transpose(T.t96[:, 0:96], T.ys[:, 0:96]))
-    T96 = R("t96", 0, 96)
-    D = lambda k: R("dd", 96 * k, 96 * k + 96)
-    C = lambda k: R("cmp", 96 * k, 96 * k + 96)
+    D = lambda k, a, b: R("dd", 96 * k + a, 96 * k + b)
+    C = lambda k, a, b: R("cmp", 96 * k + a, 96 * k + b)
+    CC = lambda k, a, b: R("cc", 96 * k + a, 96 * k + b)
     st = lambda k: R("ys", 32 * k, 32 * k + 1)
     rk = lambda k: R("rk", k, k + 1)
-    for k in (1, 2):
-        act(D(k), T96, F.Identity, -1.0, st(k))
-    ts(D(0), T96, st(0), -1.0, A.subtract, A.mult)
-    for k in range(3):
-        tt(C(k), D(k), R("cc", 96 * k, 96 * k + 96), A.is_lt)
-    shrink(0, 0)
+
+    def turn(a, b):
+        op("v", [R("ys", a, b)], [R("t96", a, b)], lambda: g.vector.transpose(T.t96[:, a:b], T.ys[:, a:b]))
+
+    def less(k, a, b):
+        act(D(k, a, b), R("t96", a, b), F.Identity, -1.0, st(k))
+
     for k in (0, 1):
-        act(R("junk", 96 * k, 96 * k + 96), C(k), F.Copy, acc=rk(k))
-    red(rk(2), C(2), A.add)
-    for k in (0, 2, 1):
-        ts(R("at", k, 512, 4), RP, rk(k), None, A.is_equal)
-    cp(R("at", 516, 528, 4), R("rk", 0, 3))
-    qz("dxw", 384, 132, "at")
+        mm("ps%d" % k, "mq", 128 * k, "prq", 0, 128)
+    product(0, 0)
+    for k in (0, 1):
+        act(R("ys", 32 * k, 32 * k + 32), R("ps%d" % k, 0, 32), F.Abs)
+    mm("ps4", "mq", 256, "prq", 0, 128)
     for i in (1, 2, 3):
-        shrink(0, i)
-    qz("dxw", 0, 256, "dxt")
-    mm("ps4", "dxw", 384, "blq", 0, 128, True, False)
-    mm("ps4", "dxw", 384, "blq", 16, 128, False, True)
+        product(0, i)
+    turn(0, 64)
+    shrink("v", 0, 0)
+    for k in (0, 1):
+        less(k, 0, 64)
+    tt(C(0, 0, 64), D(0, 0, 64), CC(0, 0, 64), A.is_lt)
+    act(R("ys", 64, 96), R("ps4", 0, 32), F.Abs)
     for i in range(4):
-        shrink(1, i)
-    cp(R("of2", 0, 12), R("ps4", 0, 12))
+        product(1, i)
+    turn(64, 96)
+    for k in (0, 1):
+        less(k, 64, 96)
+    ts(D(2, 0, 96), R("t96", 0, 96), st(2), -1.0, A.subtract, A.mult)
+    tt(C(1, 0, 64), D(1, 0, 64), CC(1, 0, 64), A.is_lt)
+    for k in (0, 1):
+        tt(C(k, 64, 96), D(k, 64, 96), CC(k, 64, 96), A.is_lt)
+    tt(C(2, 0, 96), D(2, 0, 96), CC(2, 0, 96), A.is_lt)
+    shrink("s", 0, 1)
+    for k in (0, 1):
+        act(R("junk", 96 * k, 96 * k + 96), C(k, 0, 96), F.Copy, acc=rk(k))
+    red(rk(2), C(2, 0, 96), A.add)
+    for k in (0, 1, 2):
+        ts(R("at", k, 512, 4), RP, rk(k), None, A.is_equal)
+    ts(R("at", 516, 528, 4), R("rk", 0, 3), 16.0, None, A.min)
+    qz("dxw", 384, 132, "at")
+    ahead = lambda d: 512
+    send("dxw", ahead, 4, "rv", "rkc", True, peers)
+    send("dxw_s", ahead, 4, "rv_s", "rkp", False, peers)
+    localcopy("dxw", 512, "rv", 4 * q, 4, "okc", True)
+    localcopy("dxw_s", 512, "rv_s", 4 * q, 4, "okp", False)
+    arrives("rv", 4, "rkc")
+    arrives("rv_s", 4, "rkp")
+    mm("ps2", "dxw", 384, "blq", 0, 128, True, False)
+    mm("ps2", "dxw", 384, "blq", 16, 128, False, True)
+    shrink("s", 0, 2)
+    shrink("s", 0, 3)
+    qz("dxw", 0, 256, "dxt")
+    for i in range(3):
+        shrink("s", 1, i)
+    shrink("v", 1, 3)
     qz("dxw", 256, 128, "dxt", 1024)
-    pick("ret", 0, 192, "dxw", 516, "of2", 0)
+    cp(R("of2", 0, 12), R("ps2", 0, 12))
+    pick("ret", 0, 192, "dxw", 0, 516, "of2", 0)
 
-    back = lambda d: 24 * d if d % 2 == 0 else 24 * d + 4
-    send("ret", back, 20, "rl", "rec", True, peers)
-    send("ret_s", back, 20, "rl_s", "rep", False, peers)
-    localcopy("ret", back(q), "rl", 20 * q, 20, "orc", True)
-    localcopy("ret_s", back(q), "rl_s", 20 * q, 20, "orp", False)
-    arrives("rl", 20, "rec")
-    arrives("rl_s", 20, "rep")
-    first, ranks = (0, 17) if q % 2 == 0 else (4, 1)
+    back = lambda d: 24 * d if d % 2 == 0 else 24 * d + 6
+    send("ret", back, 18, "rl", "rec", True, peers)
+    send("ret_s", back, 18, "rl_s", "rep", False, peers)
+    localcopy("ret", back(q), "rl", 18 * q, 18, "orc", True)
+    localcopy("ret_s", back(q), "rl_s", 18 * q, 18, "orp", False)
+    arrives("rl", 18, "rec")
+    arrives("rl_s", 18, "rep")
+    first = 0 if q % 2 == 0 else 2
 
-    ts(k3("mm_"), k3("mp"), MAGIC1, MAGIC1, A.add, A.subtract)
-    act(k3("m16"), k3("mm_"), F.Copy, -16.0)
-    act(k3("m20"), k3("mm_"), F.Identity, 1.0, -20.0)
     for k in range(3):
-        ts(R("oh", 128 * k, 128 * k + 128), TI, R("tok", k, k + 1), None, A.is_equal)
-    for k in range(3):
-        tt(R("oht", k, 512, 4), R("oh", 128 * k, 128 * k + 128), R("wt", 0, 128), A.mult)
         act(R("junk", 128 * k, 128 * k + 128), R("oht", k, 512, 4), F.Copy, acc=R("wk", k, k + 1))
-    act(k3("w20"), k3("wk"), F.Copy, 20.0)
-    tt(k3("rr_"), k3("m16"), k3("tok"), A.add)
-    ts(eh, eF, 8.0, None, A.subtract)
-    ts(qsel, eF, float(q), None, A.is_equal)
+    act(k3("w18"), k3("wk"), F.Copy, 18.0)
     for k in range(3):
-        ts(R("aht", 576 + k, 1088, 4), RP, R("rr_", k, k + 1), None, A.is_equal)
-        act(R("aht", 64 + k, 576, 4), R("aht", 576 + k, 1088, 4), F.Copy, 20.0)
-    ts(R("kt", 0, 512, 4), RP, iF, qsel, A.is_equal, A.mult)
-    ts(R("kt", 3, 512, 4), E128, pF, None, A.is_equal)
-    qz("rl", 160, 128, "zer")
-    qz("kq", 0, 128, "kt")
-    tt(k3("cd"), k3("w20"), k3("m20"), A.add)
+        ts(R("aht", 128 + k, 640, 4), RP, R("rr_", k, k + 1), None, A.is_equal)
+    tt(k3("cd"), k3("w18"), k3("m18"), A.add)
     for k in range(3):
         ts(R("aht", k, 64, 4), R("cp16", 0, 16), R("cd", k, k + 1), eh, A.is_equal, A.mult)
-        ts(R("mka", 16 * k, 16 * k + 16), R("cp16", 0, 16), R("cd", k, k + 1), None, A.is_equal)
-    qz("ahq", 0, 272, "aht")
-    qz("ohq", 0, 128, "oht")
-    qz("vq", 0, 128, "vb")
-    mm("ps1", "ahq", 16, "ahq", 0, 128, True, False)
-
-    mm("ps0", "kq", 0, "rl", 0, 160)
+        ts(R("aht", 64 + k, 128, 4), R("cp16", 0, 16), R("cd", k, k + 1), el, A.is_equal, A.mult)
+    qz("ahq", 0, 160, "aht")
+    mm("ps0", "kq", 0, "rv", 0, 128)
+    mm("ps1", "ahq", 32, "ahq", 0, 128, True, False)
+    mm("ps1", "ahq", 32, "ahq", 16, 128, False, False)
     for k in range(3):
-        red(R("rkh", k, k + 1), R("ps0", ranks + k, 160, 20), A.min)
+        red(R("rkh", k, k + 1), R("ps0", 1 + k, 32, 4), A.min)
     for k in range(3):
-        ts(R("bt2", k, 64, 4), R("mka", 16 * k, 16 * k + 16), R("rkh", k, k + 1), 16.0, A.mult, A.min)
+        ts(R("bt2", k, 64, 4), R("cp16", 0, 16), R("cd", k, k + 1), R("rkh", k, k + 1), A.is_equal, A.mult)
     qz("btq", 0, 128, "bt2")
-    mm("ps1", "ahq", 144, "btq", 0, 128, False, True)
-    ts(R("of3", 0, 16), R("ps1", 0, 16), 160.0 + first, None, A.add)
+    mm("ps1", "ahq", 32, "btq", 0, 128, False, True)
+    qz("ohq", 0, 128, "oht")
+    ts(R("of3", 0, 16), R("ps1", 0, 16), 144.0 + first, None, A.add)
+
     for h in range(2):
-        pick("zc", 128 * h, 128, "rl", 168, "of3", 8 * h)
+        pick("zc", 128 * h, 128, "rl", 0, 152, "of3", 8 * h)
         for b in range(4):
             mm("ps%d" % (4 + b), "ebq", 128 * b, "zc", 128 * h, 128, h == 0, h == 1)
     ts(R("bt2", 64, 67), k3("rkh"), 15.5, None, A.is_lt)
@@ -498,7 +519,7 @@ def rank_program(g, core, T, topo):
     for b in (1, 3):
         cp(R("zt", b, 512, 4), R("ps%d" % (4 + b), 0, 128))
     qz("zq", 0, 128, "zt")
-    mm("ps3", "vq", 0, "zq", 0, 128)
+    mm("ps3", "rv", 32, "zq", 0, 128)
     act(R("ctsb", 0, 128), R("ps2", 0, 128), F.Copy)
     dma("y", [R("zq", 0, 128)], [], T.oc[:, :], T.zq[:, 0:128].bitcast(dt.uint8), "o_oc")
     for k in range(4):

from concourse.bass import DstId, RemoteDMATransfer
from concourse.mybir import dt, AluOpType, AxisListType, ActivationFunctionType

A = AluOpType
F = ActivationFunctionType
BIG, FLOOR, TINY, MAGIC16, MAGIC1 = 1e29, -1e25, 2.0 ** -100, 1.5 * 2.0 ** 27, 1.5 * 2.0 ** 23

SCRATCH = {}
ALIAS = {}


def _sb(name, n, d="float32"):
    SCRATCH[name] = ("sbuf", [128, n], d)


def _mx(name, n):
    _sb(name, n, "float8_e4m3fn_x4")
    _sb(name + "_s", n, "uint8")


for _n, _w in (("xq", 664), ("tkq", 128), ("rq", 128), ("sl", 768), ("ld", 768), ("xg", 768), ("wq", 512),
               ("uq", 512), ("prq", 128), ("ebq", 512), ("mq", 384), ("dxw", 516), ("blq", 144), ("ret", 192), ("rl", 152), ("rv", 160),
               ("kq", 128), ("ahq", 160), ("ohq", 128), ("btq", 128), ("ctq", 128), ("zc", 256), ("zq", 128)):
    _mx(_n, _w)
for _n, _w in (("xt", 576), ("gt", 544), ("tri", 512), ("tk", 512), ("br", 704), ("wb", 2048), ("ubb", 2048), ("bv", 640),
               ("pb", 4), ("bp", 640), ("eye", 520), ("mt", 1536), ("dxt", 1536), ("at", 528), ("aht", 640),
               ("oht", 512), ("zt", 512), ("ti", 128), ("e128", 128), ("rp", 128), ("tmpc", 128), ("oa", 384),
               ("oh", 384), ("mk", 1536), ("sg", 768), ("junk", 384), ("dd", 288), ("cmp", 288), ("cc", 288)):
    _sb(_n, _w, "bfloat16")
for _n, _w in (("sc", 32), ("pm", 40), ("cm", 16), ("ab", 8), ("iab", 4), ("acc", 4), ("n48", 48), ("ys", 96), ("t96", 96),
               ("rk", 4), ("tok", 4), ("nt", 4), ("mp", 4), ("mm_", 4), ("m16", 4), ("m18", 4), ("rr_", 4), ("wk", 4), ("w18", 4),
               ("cd", 4), ("rkh", 4), ("ysb", 128), ("ctsb", 128)):
    _sb(_n, _w)
_at = 0
for _n, _w in (("em16", 16), ("emv", 16), ("g48", 48), ("bi", 16), ("bib", 16), ("d16", 16), ("cp16", 16), ("s96", 96), ("h96", 96),
               ("o96", 96), ("fx", 48)):
    ALIAS[_n] = ("cs", _at)
    _at += _w
_sb("cs", _at)
for _n, _b, _o in (("bt", "br", 0), ("rst", "br", 192), ("blt", "bp", 0), ("prt", "bp", 128), ("bt2", "bv", 0)):
    ALIAS[_n] = (_b, _o)
_sb("pi", 8, "int32")
for _n, _w in (("off", 48), ("ofs", 48), ("of2", 16), ("of3", 16)):
    _sb(_n, _w, "uint16")
for _k in range(8):
    SCRATCH["ps%d" % _k] = ("psum", [128, 512], "float32")
SEMAPHORES = ["sv", "ss", "st", "sg", "lx", "lrt", "lgr", "lpr", "lw", "lub", "lv", "arc", "arp", "owc", "owp", "rec", "rep", "orc", "orp",
              "rkc", "rkp", "okc", "okp", "zrc", "zrp", "loc", "o_oc", "o_y", "o_ct", "o_s0", "o_s1", "o_s2", "o_s3"]


def rank_program(g, core, T, topo):
    q = T.rank_of(core)
    if q is None:
        return
    N = len(T.cores)
    eng = {"v": g.vector, "s": g.scalar, "t": g.tensor, "g": g, "y": g.sync}
    own = {"v": "sv", "s": "ss", "t": "st", "g": "sg"}
    total, snaps, log = {}, {}, {}
    seen = {k: {} for k in eng}

    def clash(a, b):
        if a[2] <= b[1] or b[2] <= a[1]:
            return False
        return not (a[3] == b[3] > 1 and (a[1] - b[1]) % a[3])

    def wait(qn, s, v):
        if seen[qn].get(s, 0) >= v:
            return
        eng[qn].wait_ge(T.sem[s], v)
        seen[qn][s] = v
        for k, w in snaps.get((s, v), {}).items():
            seen[qn][k] = max(seen[qn].get(k, 0), w)

    def depend(qn, reads, writes, dma=False):
        need = {}
        for acc, w in [(r, False) for r in reads] + [(r, True) for r in writes]:
            bank = acc[0][:2] == "ps" and len(acc[0]) == 3
            for rec in log.get(acc[0], []):
                if not bank and not clash(acc, rec[0]):
                    continue
                if not (w or rec[1] or (bank and rec[2] != qn)):
                    continue
                if rec[2] == qn and not dma and (not rec[1] or (qn == "t" and bank)):
                    continue
                need[rec[3]] = max(need.get(rec[3], 0), rec[4])
        for s, v in need.items():
            wait(qn, s, v)

    def note(who, reads, writes, s, v):
        for r in writes:
            if r[3] == 1:
                log[r[0]] = [k for k in log.get(r[0], []) if not (r[1] <= k[0][1] and k[0][2] <= r[2])]
        for acc, w in [(r, False) for r in reads] + [(r, True) for r in writes]:
            log.setdefault(acc[0], []).append((acc, w, who, s, v))

    def op(qn, reads, writes, call):
        depend(qn, reads, writes)
        s = own[qn]
        call().then_inc(T.sem[s], 1)
        total[s] = total.get(s, 0) + 1
        snaps[(s, total[s])] = dict(seen[qn])
        note(qn, reads, writes, s, total[s])

    def dma(qn, reads, writes, out, in_, s):
        depend(qn, reads, writes, dma=True)
        eng[qn].dma_start(out, in_).then_inc(T.sem[s], 16)
        total[s] = total.get(s, 0) + 16
        snaps[(s, total[s])] = dict(seen[qn])
        note("dma", reads, writes, s, total[s])

    def R(name, lo, hi, step=1):
        b, o = ALIAS.get(name, (name, 0))
        return (b, lo + o, hi + o, step)

    def ap(r):
        return T[r[0]][:, r[1]:r[2]] if r[3] == 1 else T[r[0]][:, r[1]:r[2]:r[3]]

    def sc_(v):
        return ap(v) if isinstance(v, tuple) else v

    def rds(*vs):
        return [v for v in vs if isinstance(v, tuple)]

    def ts(out, in0, s1, s2, op0, op1=None):
        if op1 is None:
            op("v", rds(in0, s1), [out], lambda: g.vector.tensor_scalar(ap(out), ap(in0), sc_(s1), None, op0))
        else:
            op("v", rds(in0, s1, s2), [out], lambda: g.vector.tensor_scalar(ap(out), ap(in0), sc_(s1), sc_(s2), op0, op1))

    def tt(out, a, b, o):
        op("v", [a, b], [out], lambda: g.vector.tensor_tensor(ap(out), ap(a), ap(b), o))

    def cp(out, a):
        op("v", [a], [out], lambda: g.vector.tensor_copy(ap(out), ap(a)))

    def ms(out, c):
        op("v", [], [out], lambda: g.vector.memset(ap(out), c))

    def red(out, a, o):
        op("v", [a], [out], lambda: g.vector.tensor_reduce(ap(out), ap(a), AxisListType.X, o))

    def scan(out, a, z, o0, o1):
        op("v", [a, z], [out], lambda: g.vector.tensor_tensor_scan(ap(out), ap(a), ap(z), -9e29, o0, o1))

    def qz(name, lo, n, tile, t0=0):
        r = R(tile, t0, t0 + 4 * n)
        op("v", [r], [R(name, lo, lo + n), R(name + "_s", lo, lo + n)],
           lambda: g.vector.quantize_mx(T[name][:, lo:lo + n], T[name + "_s"][:, lo:lo + n], ap(r)))

    def act(out, a, f, scale=1.0, bias=0.0, acc=None):
        if acc is None:
            op("s", rds(a, scale, bias), [out], lambda: g.scalar.activation(ap(out), ap(a), f, bias=sc_(bias), scale=sc_(scale)))
        else:
            op("s", rds(a, scale, bias), [out, acc],
               lambda: g.scalar.activation(ap(out), ap(a), f, bias=sc_(bias), scale=sc_(scale), accum_out=ap(acc)))

    def zero(name, lane, hi=512, lo=0):
        act(R(name, lo + lane, hi, 4), R("ti", 0, 128), F.Copy, 0.0)

    def mm(bank, lhs, l0, rhs, r0, n, start=True, stop=True):
        op("t", [R(lhs, l0, l0 + 128), R(lhs + "_s", l0, l0 + 128), R(rhs, r0, r0 + n), R(rhs + "_s", r0, r0 + n)], [R(bank, 0, n)],
           lambda: g.tensor.matmul_mx(T[bank][:, 0:n], T[lhs][:, l0:l0 + 128], T[lhs + "_s"][:, l0:l0 + 128],
                                      T[rhs][:, r0:r0 + n], T[rhs + "_s"][:, r0:r0 + n], start, stop))

    def pickc(out, o0, n, win, w0, w1, off, f0):
        fr = R(off, f0, f0 + n // 16)
        op("v", [R(win, w0, w1), fr], [R(out, o0, o0 + n)],
           lambda: g.vector.tensor_copy(T[out][:, o0:o0 + n].bitcast(dt.uint32), T[win][:, w0:w1].bitcast(dt.uint32).indirect(ap(fr))))

    def picks(out, o0, n, win, w0, w1, off, f0):
        fr = R(off, f0, f0 + n // 16)
        op("s", [R(win + "_s", w0, w1), fr], [R(out + "_s", o0, o0 + n)],
           lambda: g.scalar.activation(T[out + "_s"][:, o0:o0 + n], T[win + "_s"][:, w0:w1].indirect(ap(fr)), F.Copy))

    def pick(*a):
        pickc(*a)
        picks(*a)

    def iota(name, n, pattern, cm=0):
        r = R(name, 0, n)
        op("g", [], [r], lambda: g.iota(ap(r), pattern, 0, cm, allow_small_or_imprecise_dtypes=True))

    peers = [c for c in T.cores if c != core]
    far = [c for c in peers if topo.die(c) != topo.die(core)]
    near = [c for c in peers if c not in far]
    masks = {}
    for group, first in ((far, 0), (near, 1)):
        for j, c in enumerate(group):
            e = topo.engines(core, c)[first::2]
            masks[c] = (1 << e[2 * j]) | (1 << e[2 * j + 1])

    def send(src, start, width, dst, s, code, to):
        blocks = [R(src, start(T.rank_of(c)), start(T.rank_of(c)) + width) for c in to]
        depend("g", blocks, [])
        ts_ = []
        for c, r in zip(to, blocks):
            rid, pid = topo.addr(c)[:2]
            a, b = ap(r), T[dst][:, width * q:width * q + width]
            if code:
                a, b = a.bitcast(dt.uint8), b.bitcast(dt.uint8)
            ts_.append(RemoteDMATransfer(dst_ids=[DstId(rid=rid, pnc=pid)], dma_engine_mask=masks[c], remote_sem=T.sem[s], src=a, dst=b))
        g.remote_dma_fused(ts_, local_sem=T.sem["loc"])
        total["loc"] = total.get("loc", 0) + 2 * len(to)
        note("dma", blocks, [], "loc", total["loc"])

    def arrives(dst, dw, s):
        total[s] = 2 * len(peers)
        for e in range(N):
            if e != q:
                note("dma", [], [R(dst, dw * e, dw * (e + 1))], s, total[s])

    def localcopy(src, a, dst, b, width, s, code):
        i, o = T[src][:, a:a + width], T[dst][:, b:b + width]
        if code:
            i, o = i.bitcast(dt.uint8), o.bitcast(dt.uint8)
        dma("y", [R(src, a, a + width)], [R(dst, b, b + width)], o, i, s)

    def load(qn, name, w, src, s, at=0):
        r = R(name, at, at + w)
        dma(qn, [], [r], ap(r), src, s)

    load("y", "xt", 512, T.x[:, :], "lx")
    load("s", "xt", 32, T.rt[:, 0:32], "lrt", 544)
    load("y", "gt", 512, T.gr[:, :], "lgr")
    load("s", "pb", 4, T.pr[:, 0:4], "lpr")
    load("y", "wb", 2048, T.w[:, :], "lw")
    load("s", "ubb", 2048, T.ub[:, :], "lub")
    load("y", "bv", 512, T.v[:, :], "lv", 128)

    iota("pi", 1, [[1, 1]], cm=1)
    iota("ti", 128, [[1, 128]])
    iota("rp", 128, [[0, 8], [1, 16]])
    iota("bi", 3, [[16, 3]])
    iota("em16", 16, [[1, 8], [0, 2]])
    iota("g48", 48, [[1, 8], [100, 2], [0, 3]])
    iota("e128", 128, [[1, 8], [0, 16]])
    iota("fx", 48, [[16, 3], [48, 2], [96, 8]])
    iota("d16", 12, [[32, 4], [8, 3]])
    iota("s96", 96, [[16, 3], [0, 2], [1, 16]])
    iota("h96", 96, [[0, 3], [1, 2], [0, 16]])
    iota("cp16", 16, [[18, 2], [1, 8]])
    iota("blt", 128, [[0, 128]])
    col = lambda k: R("sc", k, k + 1)
    pF, iF, eF, hF, e100, iH, flag, e16, eh, el, qsel = [col(k) for k in (0, 1, 2, 3, 5, 6, 7, 8, 12, 13, 14)]
    TI, RP, E128 = R("ti", 0, 128), R("rp", 0, 128), R("e128", 0, 128)
    p0 = R("pi", 0, 1)
    ms(R("xt", 512, 544), 0.0)
    ms(R("pm", 0, 40), FLOOR)
    ms(R("gt", 512, 544), 0.0)
    ts(R("pi", 1, 2), p0, 15, None, A.bitwise_and)
    ts(R("pi", 2, 3), p0, 4, None, A.arith_shift_right)
    ts(R("pi", 3, 4), p0, 4, 1, A.arith_shift_right, A.bitwise_and)
    ms(R("eye", 0, 520), 0.0)
    cp(R("sc", 0, 4), R("pi", 0, 4))
    ts(R("eye", 4, 516, 4), TI, pF, None, A.is_equal)
    for lane in range(4):
        ts(R("tri", lane, 512, 4), TI, pF, None, A.is_ge)
    for lane in range(4):
        ts(R("rst", lane, 512, 4), RP, iF, None, A.is_equal)
    zero("tk", 2)
    zero("tk", 3)
    zero("oht", 3)
    zero("aht", 3, 640, 128)
    act(R("aht", 0, 128), TI, F.Copy, 0.0)
    act(e100, eF, F.Identity, 1.0, 100.0)
    act(iH, iF, F.Identity, 1.0, 0.5)
    act(e16, eF, F.Copy, 16.0)
    act(R("bib", 0, 3), R("bi", 0, 3), F.Identity, 1.0, iH)
    qz("xq", 128, 144, "xt")
    mm("ps0", "xq", 128, "xq", 144, 128)
    qz("xq", 272, 128, "tri")
    qz("ebq", 0, 128, "eye", 4)
    ts(R("bt", 2, 192, 4), R("g48", 0, 48), e100, 512.0, A.is_equal, A.mult)
    act(R("bt", 3, 192, 4), R("bt", 2, 192, 4), F.Copy, 0.0625)

    S = R("ps0", 120, 128)
    ts(R("emv", 0, 16), R("em16", 0, 16), eF, None, A.is_equal)
    scan(R("pm", 1, 9), S, R("pm", 32, 40), A.max, A.max)
    act(R("junk", 0, 8), R("pm", 1, 9), F.Sign, -1.0, R("pm", 8, 9), R("iab", 0, 1))
    ts(R("cm", 0, 8), R("pm", 1, 9), R("pm", 8, 9), BIG, A.is_lt, A.mult)
    tt(R("ab", 0, 8), R("cm", 0, 8), R("pm", 0, 8), A.add)
    scan(R("pm", 17, 25), S, R("ab", 0, 8), A.max, A.min)
    act(R("junk", 8, 16), R("pm", 17, 25), F.Sign, -1.0, R("pm", 24, 25), R("iab", 1, 2))
    ts(R("tk", 0, 512, 4), E128, R("iab", 0, 1), None, A.is_equal)
    ts(R("tk", 1, 512, 4), E128, R("iab", 1, 2), None, A.is_equal)
    qz("tkq", 0, 128, "tk")

    k3 = lambda n: R(n, 0, 3)
    mm("ps1", "tkq", 0, "xq", 270, 130)
    mm("ps2", "tkq", 0, "xq", 270, 130)
    qz("rq", 0, 128, "rst")
    qz("xq", 400, 136, "gt")
    qz("ebq", 128, 128, "eye", 3)
    for k in range(2):
        act(R("junk", 16 + 128 * k, 144 + 128 * k), R("ps1", 2, 130), F.Sign, -1.0, R("bib", k, k + 1), R("acc", k, k + 1))
    ts(R("tmpc", 0, 128), R("ps2", 2, 130), R("bib", 2, 3), 0.5, A.is_lt, A.subtract)
    ts(R("ofs", 0, 48), R("fx", 0, 48), iF, None, A.add)
    red(R("acc", 2, 3), R("tmpc", 0, 128), A.add)
    for k in range(2):
        act(R("n48", k, 48, 3), R("emv", 0, 16), F.Copy, R("acc", k, k + 1))
    ts(R("prt", 0, 512, 4), TI, 0.0, R("pb", 0, 1), A.mult, A.add)
    ts(R("n48", 2, 48, 3), R("emv", 0, 16), R("acc", 2, 3), 2.0, A.mult, A.mult)
    ts(R("prt", 1, 512, 4), TI, 0.0, R("pb", 1, 2), A.mult, A.add)
    ts(R("bt", 0, 192, 4), R("n48", 0, 48), MAGIC16, MAGIC16, A.add, A.subtract)
    ts(R("prt", 2, 512, 4), TI, 0.0, R("pb", 2, 3), A.mult, A.add)
    tt(R("bt", 1, 192, 4), R("n48", 0, 48), R("bt", 0, 192, 4), A.subtract)
    ts(R("prt", 3, 512, 4), TI, 0.0, R("pb", 3, 4), A.mult, A.add)
    qz("xq", 536, 128, "bt")
    mm("ps4", "rq", 0, "xq", 526, 128)
    for b in (2, 3):
        qz("ebq", 128 * b, 128, "eye", 4 - b)
    ts(R("off", 0, 48), R("ps4", 10, 58), 0.5, 64.0, A.mult, A.add)
    act(R("s96", 0, 96), R("s96", 0, 96), F.Copy, -TINY)
    act(R("sc", 9, 12), R("bib", 0, 3), F.Identity, TINY, -0.5 * TINY)
    act(R("tok", 0, 2), R("acc", 0, 2), F.Identity, 0.5, 64.0)
    act(R("tok", 2, 3), R("acc", 2, 3), F.Identity, 1.0, 64.0)
    act(k3("nt"), k3("tok"), F.Copy, -1.0)
    act(k3("mp"), k3("tok"), F.Identity, 0.0625, -0.46875)
    for k in range(3):
        act(R("oa", 128 * k, 128 * k + 128), TI, F.Abs, 1.0, R("nt", k, k + 1))

    there = [T.rank_of(c) for c in far]
    for group in (there[:2], there[2:], [e for e in range(N) if e not in there]):
        for e in group:
            if e - 1 not in group:
                n = 1
                while e + n in group:
                    n += 1
                pick("sl", 96 * e, 96 * n, "xq", 128, 536, "off", 6 * e)
    out = lambda e: 96 * e
    for to in (far[:2], far[2:], near):
        send("sl", out, 96, "ld", "arc", True, to)
    send("sl_s", out, 96, "ld_s", "arp", False, peers)
    localcopy("sl", 96 * q, "ld", 96 * q, 96, "owc", True)
    localcopy("sl_s", 96 * q, "ld_s", 96 * q, 96, "owp", False)
    localcopy("xq", 256, "rl", 144, 8, "zrc", True)
    localcopy("xq_s", 256, "rl_s", 144, 8, "zrp", False)
    arrives("ld", 96, "arc")
    arrives("ld_s", 96, "arp")

    iota("bt2", 128, [[0, 128]])
    qz("prq", 0, 128, "prt")
    ts(R("tri", 0, 512, 4), TI, pF, None, A.is_equal)
    ts(R("tri", 1, 512, 4), TI, pF, 2.0, A.is_equal, A.mult)
    ts(R("o96", 0, 96), R("h96", 0, 96), hF, -BIG, A.not_equal, A.mult)
    ts(R("at", 3, 512, 4), RP, pF, None, A.is_equal)
    qz("xq", 0, 128, "tri")
    ms(R("at", 512, 528), 0.0)
    ts(flag, pF, float(q), 64.0, A.not_equal, A.mult)
    tt(R("o96", 0, 96), R("o96", 0, 96), R("s96", 0, 96), A.add)
    D16 = R("d16", 0, 12)
    ts(R("blt", 1, 48, 4), D16, e16, 128.0, A.is_equal, A.mult)
    ts(R("blt", 64, 112, 4), D16, e16, iF, A.is_equal, A.mult)
    mm("ps3", "tkq", 0, "xq", 0, 130)
    for k in range(3):
        act(R("oh", 128 * k, 128 * k + 128), R("oa", 128 * k, 128 * k + 128), F.Relu, -1.0, 1.0)
    act(R("blt", 2, 48, 4), R("blt", 1, 48, 4), F.Copy, 2.0)
    act(R("blt", 3, 48, 4), D16, F.Copy)
    for k in (1, 2):
        act(R("blt", 64 + k, 112, 4), R("blt", 64, 112, 4), F.Copy)
    act(R("at", 517, 528, 4), R("ti", 0, 3), F.Identity, 0.0, flag)
    for k in range(3):
        act(R("cc", 96 * k, 96 * k + 96), R("o96", 0, 96), F.Identity, 1.0, col(9 + k))
    qz("wq", 0, 512, "wb")
    ms(R("blt", 7, 48, 12), 512.0)
    ts(k3("mm_"), k3("mp"), MAGIC1, MAGIC1, A.add, A.subtract)
    for k in range(3):
        tt(R("oht", k, 512, 4), R("ps3", 0, 128), R("oh", 128 * k, 128 * k + 128), A.mult)
    qz("uq", 0, 512, "ubb")
    qz("blq", 0, 144, "blt")
    act(k3("m16"), k3("mm_"), F.Copy, -16.0)
    act(k3("m18"), k3("mm_"), F.Identity, 1.0, -18.0)
    ts(qsel, eF, float(q), None, A.is_equal)
    ts(eh, eF, 8.0, 16.0, A.subtract, A.mult)
    ts(el, eF, 8.0, 2.0, A.subtract, A.mult)
    ts(R("tk", 1, 512, 4), E128, pF, None, A.is_equal)
    ts(R("tk", 0, 512, 4), RP, iF, qsel, A.is_equal, A.mult)
    tt(k3("rr_"), k3("m16"), k3("tok"), A.add)
    qz("rv", 32, 128, "bv", 128)
    qz("kq", 0, 128, "tk")

    MK = lambda b, o: R("mk", 384 * b + o, 384 * b + o + 128)
    pick("xg", 0, 128, "ld", 0, 768, "ofs", 0)
    pick("xg", 128, 128, "ld", 0, 768, "ofs", 8)
    pick("xg", 256, 256, "ld", 0, 768, "ofs", 16)
    pickc("xg", 512, 256, "ld", 0, 768, "ofs", 32)
    for o in (0, 128, 256):
        for i in range(4):
            mm("ps%d" % i, "wq", 128 * i, "xg", 2 * o, 128)
        for b in range(4):
            mm("ps%d" % (4 + b), "ebq", 128 * b, "xg", 2 * o + 128, 128)
        for b in (0, 2):
            ts(MK(b, o), R("ps%d" % b, 0, 128), 0.0, None, A.is_gt)
        for j, b in enumerate((1, 3)):
            act(R("sg", 384 * j + o, 384 * j + o + 128), R("ps%d" % b, 0, 128), F.Sign)
            act(MK(b, o), R("sg", 384 * j + o, 384 * j + o + 128), F.Relu)
        if o == 0:
            picks("xg", 512, 256, "ld", 0, 768, "ofs", 32)
        for b in range(4):
            tt(R("mt", 4 * o + b, 4 * o + 512, 4), R("ps%d" % (4 + b), 0, 128), MK(b, o), A.mult)
        qz("mq", o, 128, "mt", 4 * o)

    parts = ((0, 256), (256, 128))
    UB = (("ps2", "ps3", "ps5", "ps6"), ("ps7", "ps0", "ps1", "ps4"))

    def product(h, i):
        mm(UB[h][i], "uq", 128 * i, "mq", parts[h][0], parts[h][1])

    def shrink(qn, h, i):
        o, n = parts[h]
        if qn == "s":
            act(R("dxt", 4 * o + i, 4 * (o + n), 4), R(UB[h][i], 0, n), F.Copy, 0.0625)
        else:
            ts(R("dxt", 4 * o + i, 4 * (o + n), 4), R(UB[h][i], 0, n), 0.0625, None, A.mult)

    D = lambda k, a, b: R("dd", 96 * k + a, 96 * k + b)
    C = lambda k, a, b: R("cmp", 96 * k + a, 96 * k + b)
    CC = lambda k, a, b: R("cc", 96 * k + a, 96 * k + b)
    st = lambda k: R("ys", 32 * k, 32 * k + 1)
    rk = lambda k: R("rk", k, k + 1)

    def turn(a, b):
        op("v", [R("ys", a, b)], [R("t96", a, b)], lambda: g.vector.transpose(T.t96[:, a:b], T.ys[:, a:b]))

    def less(k, a, b):
        act(D(k, a, b), R("t96", a, b), F.Identity, -1.0, st(k))

    for k in (0, 1):
        mm("ps%d" % k, "mq", 128 * k, "prq", 0, 128)
    product(0, 0)
    for k in (0, 1):
        act(R("ys", 32 * k, 32 * k + 32), R("ps%d" % k, 0, 32), F.Abs)
    mm("ps4", "mq", 256, "prq", 0, 128)
    for i in (1, 2, 3):
        product(0, i)
    turn(0, 64)
    shrink("v", 0, 0)
    for k in (0, 1):
        less(k, 0, 64)
    tt(C(0, 0, 64), D(0, 0, 64), CC(0, 0, 64), A.is_lt)
    act(R("ys", 64, 96), R("ps4", 0, 32), F.Abs)
    for i in range(4):
        product(1, i)
    turn(64, 96)
    for k in (0, 1):
        less(k, 64, 96)
    ts(D(2, 0, 96), R("t96", 0, 96), st(2), -1.0, A.subtract, A.mult)
    tt(C(1, 0, 64), D(1, 0, 64), CC(1, 0, 64), A.is_lt)
    for k in (0, 1):
        tt(C(k, 64, 96), D(k, 64, 96), CC(k, 64, 96), A.is_lt)
    tt(C(2, 0, 96), D(2, 0, 96), CC(2, 0, 96), A.is_lt)
    shrink("s", 0, 1)
    for k in (0, 1):
        act(R("junk", 96 * k, 96 * k + 96), C(k, 0, 96), F.Copy, acc=rk(k))
    red(rk(2), C(2, 0, 96), A.add)
    for k in (0, 1, 2):
        ts(R("at", k, 512, 4), RP, rk(k), None, A.is_equal)
    ts(R("at", 516, 528, 4), R("rk", 0, 3), 16.0, None, A.min)
    qz("dxw", 384, 132, "at")
    ahead = lambda d: 512
    send("dxw", ahead, 4, "rv", "rkc", True, peers)
    send("dxw_s", ahead, 4, "rv_s", "rkp", False, peers)
    localcopy("dxw", 512, "rv", 4 * q, 4, "okc", True)
    localcopy("dxw_s", 512, "rv_s", 4 * q, 4, "okp", False)
    arrives("rv", 4, "rkc")
    arrives("rv_s", 4, "rkp")
    mm("ps2", "dxw", 384, "blq", 0, 128, True, False)
    mm("ps2", "dxw", 384, "blq", 16, 128, False, True)
    shrink("s", 0, 2)
    shrink("s", 0, 3)
    qz("dxw", 0, 256, "dxt")
    for i in range(3):
        shrink("s", 1, i)
    shrink("v", 1, 3)
    qz("dxw", 256, 128, "dxt", 1024)
    cp(R("of2", 0, 12), R("ps2", 0, 12))
    pick("ret", 0, 192, "dxw", 0, 516, "of2", 0)

    back = lambda d: 24 * d if d % 2 == 0 else 24 * d + 6
    send("ret", back, 18, "rl", "rec", True, peers)
    send("ret_s", back, 18, "rl_s", "rep", False, peers)
    localcopy("ret", back(q), "rl", 18 * q, 18, "orc", True)
    localcopy("ret_s", back(q), "rl_s", 18 * q, 18, "orp", False)
    arrives("rl", 18, "rec")
    arrives("rl_s", 18, "rep")
    first = 0 if q % 2 == 0 else 2

    for k in range(3):
        act(R("junk", 128 * k, 128 * k + 128), R("oht", k, 512, 4), F.Copy, acc=R("wk", k, k + 1))
    act(k3("w18"), k3("wk"), F.Copy, 18.0)
    for k in range(3):
        ts(R("aht", 128 + k, 640, 4), RP, R("rr_", k, k + 1), None, A.is_equal)
    tt(k3("cd"), k3("w18"), k3("m18"), A.add)
    for k in range(3):
        ts(R("aht", k, 64, 4), R("cp16", 0, 16), R("cd", k, k + 1), eh, A.is_equal, A.mult)
        ts(R("aht", 64 + k, 128, 4), R("cp16", 0, 16), R("cd", k, k + 1), el, A.is_equal, A.mult)
    qz("ahq", 0, 160, "aht")
    mm("ps0", "kq", 0, "rv", 0, 128)
    mm("ps1", "ahq", 32, "ahq", 0, 128, True, False)
    mm("ps1", "ahq", 32, "ahq", 16, 128, False, False)
    for k in range(3):
        red(R("rkh", k, k + 1), R("ps0", 1 + k, 32, 4), A.min)
    for k in range(3):
        ts(R("bt2", k, 64, 4), R("cp16", 0, 16), R("cd", k, k + 1), R("rkh", k, k + 1), A.is_equal, A.mult)
    qz("btq", 0, 128, "bt2")
    mm("ps1", "ahq", 32, "btq", 0, 128, False, True)
    qz("ohq", 0, 128, "oht")
    ts(R("of3", 0, 16), R("ps1", 0, 16), 144.0 + first, None, A.add)

    for h in range(2):
        pick("zc", 128 * h, 128, "rl", 0, 152, "of3", 8 * h)
        for b in range(4):
            mm("ps%d" % (4 + b), "ebq", 128 * b, "zc", 128 * h, 128, h == 0, h == 1)
    ts(R("bt2", 64, 67), k3("rkh"), 15.5, None, A.is_lt)
    qz("ctq", 0, 128, "bt2")
    mm("ps2", "ctq", 0, "ohq", 0, 128)
    for b in (0, 2):
        act(R("zt", b, 512, 4), R("ps%d" % (4 + b), 0, 128), F.Copy)
    for b in (1, 3):
        cp(R("zt", b, 512, 4), R("ps%d" % (4 + b), 0, 128))
    qz("zq", 0, 128, "zt")
    mm("ps3", "rv", 32, "zq", 0, 128)
    act(R("ctsb", 0, 128), R("ps2", 0, 128), F.Copy)
    dma("y", [R("zq", 0, 128)], [], T.oc[:, :], T.zq[:, 0:128].bitcast(dt.uint8), "o_oc")
    for k in range(4):
        dma("y" if k < 1 else "s", [R("zq_s", 0, 128)], [], T.osc[4 * k:4 * k + 4, 0:128], T.zq_s[32 * k:32 * k + 4, 0:128], "o_s%d" % k)
    dma("s", [R("ctsb", 0, 128)], [], T.ct[:, :], T.ctsb[16:17, 0:128], "o_ct")
    cp(R("ysb", 0, 128), R("ps3", 0, 128))
    dma("y", [R("ysb", 0, 128)], [], T.y[:, :], T.ysb[:, 0:128], "o_y")

    for s, v in total.items():
        wait("g", s, v)
